import numpy as np
import ml_dtypes


def mxq(x, axis, fmt="e4m3"):
    dtype, down = {"e4m3": (ml_dtypes.float8_e4m3fn, 7), "e5m2": (ml_dtypes.float8_e5m2, 14)}[fmt]
    v = np.moveaxis(np.asarray(x, np.float32).astype(ml_dtypes.bfloat16).astype(np.float64), axis, -1)
    blocks = v.reshape(v.shape[:-1] + (-1, 32))
    amax = np.abs(blocks).max(-1, keepdims=True)
    byte = np.maximum(np.where(amax > 0, np.frexp(amax)[1] - 1 + 127, 0) - down, 1)
    scale = np.exp2(byte - 127.0)
    codes = (blocks / scale).astype(np.float32).astype(dtype).astype(np.float64)
    return np.moveaxis((codes * scale).reshape(v.shape), -1, axis)


WIDE = False


def mx_kscale(k):
    if not WIDE:
        return np.ones(k)
    levels = np.array([10, -10, 5, -5, 0])
    if k % 512:
        return np.exp2(np.random.permutation(np.resize(levels, k // 32))).repeat(32)
    a = np.empty((k // 512, 16))
    for p in range(k // 512):
        a[p, :8] = np.random.permutation(np.resize(levels, 8))
        for g in range(8):
            far = levels[np.abs(levels - a[p, g]) >= 10]
            a[p, g + 8] = far[np.random.randint(len(far))]
    return np.exp2(a.ravel()).repeat(32)


def f64(x):
    return np.asarray(x).astype(np.float64)


def striped(idx):
    return np.tile(idx.reshape(-1, 16).T, (8, 1)).astype(np.uint16)


def unstriped(offs):
    return offs[:16].T.reshape(-1).astype(np.int64)


E2M1 = np.array([0.0, 0.5, 1.0, 1.5, 2.0, 3.0, 4.0, 6.0, -0.0, -0.5, -1.0, -1.5, -2.0, -3.0, -4.0, -6.0])


def pack_fp4(w):
    k, n = w.shape
    w = f64(np.asarray(w, np.float32).astype(ml_dtypes.bfloat16)).reshape(k // 32, 32, n)
    amax = np.abs(w).max(1)
    mant, ex = np.frexp(amax / 6.0)
    byte = np.clip(np.where(amax > 0, np.where(mant > 0.5, ex, ex - 1) + 127, 1), 1, 254)
    scaled = (w * np.exp2(127.0 - byte)[:, None, :]).reshape(k, n).astype(np.float32)
    c = np.ascontiguousarray(scaled.reshape(k // 512, 128, 4, n).transpose(0, 1, 3, 2)).astype(ml_dtypes.float4_e2m1fn).view(np.uint8) & 0xF
    words = (c[..., 0::2] | (c[..., 1::2] << 4)).reshape(k // 512, 128, 2 * n)
    return np.ascontiguousarray(words), np.ascontiguousarray(byte.astype(np.uint8).reshape(k // 512, 16, n))


def unpack_fp4(words, scales):
    g, _, n = scales.shape
    words = np.ascontiguousarray(words).reshape(g, 128, n, 2)
    nib = np.empty((g, 128, n, 4), np.uint8)
    nib[..., 0::2] = words & 0xF
    nib[..., 1::2] = words >> 4
    vals = E2M1[nib] * np.repeat(np.exp2(scales.astype(np.float64) - 127.0), 8, axis=1)[..., None]
    return vals.transpose(0, 1, 3, 2).reshape(g * 512, n)


def gelu(v):
    return 0.5 * v * (1.0 + np.tanh(np.sqrt(2.0 / np.pi) * (v + 0.044715 * v**3)))


K, T, S, V, N = 1024, 2048, 1024, 512, 256
P = 2 ** 7


def setup_inputs():
    n = np.random.standard_normal
    s = mx_kscale(K)[:, None]
    packed_xT = pack_fp4(n((K, T)) * s)
    return {
        "x_words": packed_xT[0],
        "x_scales": packed_xT[1],
        "w1": (n((K, N)) / np.sqrt(K) / s).astype(np.float32),
        "frac": np.tile(np.random.uniform(0.05, 0.95, V), (P, 1)).astype(np.float32),
        "offs": striped(np.random.permutation(T)[:S]),
        "left": striped(np.random.permutation(S)[:V]),
        "right": striped(np.random.permutation(S)[:V]),
    }


def reference(x_words, x_scales, w1, frac, offs, left, right):
    xq = unpack_fp4(x_words, x_scales)[:, unstriped(offs)]
    y = gelu(mxq(f64(w1), 0, "e4m3").T @ xq)
    l = y[:, unstriped(left)]
    return l + (y[:, unstriped(right)] - l) * f64(frac)[:1]

@@ -1,0 +1,157 @@
+from contextlib import ExitStack
+
+import concourse.mybir as mybir
+
+K, T, S, V, N = 1024, 2048, 1024, 512, 256
+P = 128
+PACK = 4
+PASSES = K // (P * PACK)
+BLOCKS = N // P
+FLOPS = 2 * K * N * S
+
+F32 = mybir.dt.float32
+BF16 = mybir.dt.bfloat16
+I32 = mybir.dt.int32
+U32 = mybir.dt.uint32
+U16 = mybir.dt.uint16
+U8 = mybir.dt.uint8
+FP8X4 = mybir.dt.float8_e4m3fn_x4
+FP4X4 = mybir.dt.float4_e2m1fn_x4
+ACT = mybir.ActivationFunctionType
+ALU = mybir.AluOpType
+
+
+def tile_picked_lerp_gelu_p_kernel(tc, x_words, x_scales, w1, frac, offs, left, right, out):
+    nc = tc.nc
+    with ExitStack() as ctx:
+        lists = ctx.enter_context(tc.tile_pool(name="lists", bufs=1))
+        sb = ctx.enter_context(tc.tile_pool(name="sb", bufs=1))
+        psum = ctx.enter_context(tc.psum_pool(name="psum", bufs=1))
+
+        offs_t = lists.tile([P, S // 16], U16, name="offs_t")
+        left_t = lists.tile([P, V // 16], U16, name="left_t")
+        right_t = lists.tile([P, V // 16], U16, name="right_t")
+
+        scale_win = sb.tile([P, T], U8, name="scale_win", tag="scales_then_frac", align_bytes=64)
+        nc.sync.dma_start(out=scale_win[0:32, :].bitcast(I32), in_=x_scales.rearrange("z q c -> (z q) c").bitcast(I32))
+        nc.sync.dma_start(offs_t[:], offs)
+        nc.sync.dma_start(left_t[:], left)
+        nc.sync.dma_start(right_t[:], right)
+        nc.vector.memset(scale_win[32:64, :].bitcast(I32), 0)
+        nc.vector.memset(scale_win[64:128, :].bitcast(I32), 0)
+
+        word_win = [sb.tile([P, T], U16, name=f"word_win{z}", align_bytes=64) for z in range(PASSES)]
+        w_raw = [sb.tile([P, PACK, N], F32, name=f"w_raw{z}", align_bytes=64) for z in range(PASSES)]
+        nc.sync.dma_start(out=word_win[0][:].bitcast(I32), in_=x_words[0].bitcast(I32))
+        for z in range(PASSES):
+            nc.sync.dma_start(out=w_raw[z][:], in_=w1[z * 512:(z + 1) * 512, :].rearrange("(p j) m -> p j m", j=PACK))
+        nc.sync.dma_start(out=word_win[1][:].bitcast(I32), in_=x_words[1].bitcast(I32))
+
+        warm = sb.tile([P, 8], F32, name="warm")
+        warm_out = sb.tile([P, 8], F32, name="warm_out")
+        nc.vector.memset(warm[:], 0.0)
+        nc.scalar.activation(warm_out[:], warm[:], ACT.Gelu_apprx_tanh)
+
+        x_plane = [sb.tile([P, S], U8, name=f"x_plane{z}", align_bytes=64) for z in range(PASSES)]
+        for z in range(PASSES):
+            nc.vector.memset(x_plane[z][:].bitcast(I32), 0)
+
+        picked_scales = sb.tile([P, S], U8, name="picked_scales", align_bytes=64)
+        nc.vector.tensor_copy(picked_scales[:], scale_win[:].indirect(offs_t[:]))
+        for z in range(PASSES):
+            queue = nc.scalar if z == 0 else nc.sync
+            for r in range(4):
+                queue.dma_start(out=x_plane[z][r:P:32, :].bitcast(I32),
+                                in_=picked_scales[16 * z + r:16 * z + 16:4, :].bitcast(I32))
+
+        frac_t = sb.tile([P, V], F32, name="frac_t", tag="scales_then_frac", align_bytes=64)
+        nc.sync.dma_start(out=frac_t[:], in_=frac)
+
+        pieces = [(0, 0, 512), (0, 512, 512), (1, 0, 512), (1, 512, 256), (1, 768, 256)]
+        picked = {(z, h): sb.tile([P, 512], U16, name=f"picked{z}_{h}", align_bytes=64)
+                  for z in range(PASSES) for h in range(2)}
+
+        def picked_cols(z, j0, n):
+            return picked[(z, j0 // 512)][:, j0 % 512:j0 % 512 + n]
+
+        def gather_words(z, j0, n):
+            nc.vector.tensor_copy(picked_cols(z, j0, n), word_win[z][:].indirect(offs_t[:, j0 // 16:(j0 + n) // 16]))
+
+        w_bf, w_codes, w_plane = {}, {}, {}
+
+        def cast_w(b, z):
+            t = sb.tile([P, P, PACK], BF16, name=f"w_bf{b}_{z}", align_bytes=64)
+            nc.scalar.copy(t[:].rearrange("p (c i) t -> p c t i", i=4),
+                           w_raw[z][:, :, b * P:(b + 1) * P].rearrange("p t (c i) -> p c t i", i=4))
+            w_bf[(b, z)] = t
+
+        def quantize_w(b, z):
+            codes = sb.tile([P, P], U32, name=f"w_codes{b}_{z}", align_bytes=64)
+            plane = sb.tile([P, P], U8, name=f"w_plane{b}_{z}", align_bytes=64)
+            nc.vector.quantize_mx(out=codes[:].bitcast(FP8X4), scales=plane[:],
+                                  in_=w_bf[(b, z)][:].rearrange("p m t -> p (m t)"))
+            w_codes[(b, z)], w_plane[(b, z)] = codes, plane
+
+        def mm(acc, b, z, j0, n):
+            nc.tensor.matmul_mx(out=acc, lhsT=w_codes[(b, z)][:].bitcast(FP8X4), lhsT_scale=w_plane[(b, z)][:],
+                                rhs=picked_cols(z, j0, n).bitcast(FP4X4), rhs_scale=x_plane[z][:, j0:j0 + n],
+                                start=(z == 0), stop=(z == PASSES - 1))
+
+        cast_w(0, 0)
+        cast_w(0, 1)
+        cast_w(1, 0)
+        cast_w(1, 1)
+        gather_words(*pieces[0])
+        quantize_w(0, 0)
+        gather_words(*pieces[1])
+        quantize_w(0, 1)
+        gather_words(*pieces[2])
+        quantize_w(1, 0)
+        gather_words(*pieces[3])
+        gather_words(*pieces[4])
+        quantize_w(1, 1)
+
+        rest = sb.tile([P, V], F32, name="rest", align_bytes=64)
+        nc.scalar.activation(rest[:], frac_t[:], ACT.Copy, bias=1.0, scale=-1.0)
+
+        y = [sb.tile([P, S], F32, name=f"y{b}", align_bytes=64) for b in range(BLOCKS)]
+        bank = {}
+        for b in range(BLOCKS):
+            for h in range(2):
+                bank[(b, h)] = psum.tile([P, 512], F32, name=f"bank{b}_{h}")
+        tail = [psum.tile([P, 512], F32, name=f"tail{g}") for g in range(2)]
+
+        mm(bank[(0, 0)][:], 0, 0, 0, 512)
+        for g in range(2):
+            mm(tail[g][:, 0:P], 0, 0, 768 + g * P, P)
+        mm(bank[(1, 0)][:], 1, 0, 0, 512)
+        mm(bank[(1, 1)][:], 1, 0, 512, 512)
+        mm(bank[(0, 0)][:], 0, 1, 0, 512)
+        nc.scalar.activation(y[0][:, 0:512], bank[(0, 0)][:], ACT.Gelu_apprx_tanh)
+        for g in range(2):
+            for z in range(PASSES):
+                mm(bank[(0, 1)][:, g * P:(g + 1) * P], 0, z, 512 + g * P, P)
+        nc.scalar.activation(y[0][:, 512:768], bank[(0, 1)][:, 0:256], ACT.Gelu_apprx_tanh)
+        for g in range(2):
+            mm(tail[g][:, 0:P], 0, 1, 768 + g * P, P)
+            nc.scalar.activation(y[0][:, 768 + g * P:768 + (g + 1) * P], tail[g][:, 0:P], ACT.Gelu_apprx_tanh)
+        for h in range(2):
+            mm(bank[(1, h)][:], 1, 1, h * 512, 512)
+            nc.scalar.activation(y[1][:, h * 512:(h + 1) * 512], bank[(1, h)][:], ACT.Gelu_apprx_tanh)
+
+        part_l = [sb.tile([P, V], F32, name=f"part_l{b}", align_bytes=64) for b in range(BLOCKS)]
+        part_r = [sb.tile([P, V], F32, name=f"part_r{b}", align_bytes=64) for b in range(BLOCKS)]
+        res = [sb.tile([P, V], F32, name=f"res{b}", align_bytes=64) for b in range(BLOCKS)]
+        nc.vector.tensor_tensor(part_l[0][:], y[0][:].indirect(left_t[:]), rest[:], ALU.mult)
+        nc.vector.tensor_tensor(part_r[0][:], y[0][:].indirect(right_t[:]), frac_t[:], ALU.mult)
+        nc.vector.tensor_tensor(part_l[1][:], y[1][:].indirect(left_t[:]), rest[:], ALU.mult)
+        nc.vector.tensor_tensor(res[0][:], part_l[0][:], part_r[0][:], ALU.add)
+        nc.sync.dma_start(out=out[0:P, :], in_=res[0][:])
+        half = V // 2
+        for h in range(2):
+            c = slice(h * half, (h + 1) * half)
+            nc.vector.tensor_tensor(part_r[1][:, c], y[1][:].indirect(right_t[:, h * 16:(h + 1) * 16]), frac_t[:, c], ALU.mult)
+        for h in range(2):
+            c = slice(h * half, (h + 1) * half)
+            nc.vector.tensor_tensor(res[1][:, c], part_l[1][:, c], part_r[1][:, c], ALU.add)
+            nc.sync.dma_start(out=out[P:2 * P, c], in_=res[1][:, c])

@@ -1,6 +1,7 @@
 from contextlib import ExitStack
 
 import concourse.mybir as mybir
+from concourse.masks import make_identity
 
 K, T, S, V, N = 1024, 2048, 1024, 512, 256
 P = 128
@@ -33,19 +34,22 @@ def tile_picked_lerp_gelu_p_kernel(tc, x_words, x_scales, w1, frac, offs, left, 
         right_t = lists.tile([P, V // 16], U16, name="right_t")
 
         scale_win = sb.tile([P, T], U8, name="scale_win", tag="scales_then_frac", align_bytes=64)
-        nc.sync.dma_start(out=scale_win[0:32, :].bitcast(I32), in_=x_scales.rearrange("z q c -> (z q) c").bitcast(I32))
+        nc.scalar.dma_start(out=scale_win[0:32, :].bitcast(I32), in_=x_scales.rearrange("z q c -> (z q) c").bitcast(I32))
         nc.sync.dma_start(offs_t[:], offs)
         nc.sync.dma_start(left_t[:], left)
         nc.sync.dma_start(right_t[:], right)
         nc.vector.memset(scale_win[32:64, :].bitcast(I32), 0)
         nc.vector.memset(scale_win[64:128, :].bitcast(I32), 0)
 
-        word_win = [sb.tile([P, T], U16, name=f"word_win{z}", align_bytes=64) for z in range(PASSES)]
+        word_win = [sb.tile([P, T], U16, name=f"word_win{z}", tag=f"word_win{z}", align_bytes=64) for z in range(PASSES)]
         w_raw = [sb.tile([P, PACK, N], F32, name=f"w_raw{z}", align_bytes=64) for z in range(PASSES)]
         nc.sync.dma_start(out=word_win[0][:].bitcast(I32), in_=x_words[0].bitcast(I32))
         for z in range(PASSES):
             nc.sync.dma_start(out=w_raw[z][:], in_=w1[z * 512:(z + 1) * 512, :].rearrange("(p j) m -> p j m", j=PACK))
         nc.sync.dma_start(out=word_win[1][:].bitcast(I32), in_=x_words[1].bitcast(I32))
+
+        ident = sb.tile([P, P], F32, name="ident", align_bytes=64)
+        make_identity(nc, ident[:])
 
         warm = sb.tile([P, 8], F32, name="warm")
         warm_out = sb.tile([P, 8], F32, name="warm_out")
@@ -77,23 +81,23 @@ def tile_picked_lerp_gelu_p_kernel(tc, x_words, x_scales, w1, frac, offs, left, 
         def gather_words(z, j0, n):
             nc.vector.tensor_copy(picked_cols(z, j0, n), word_win[z][:].indirect(offs_t[:, j0 // 16:(j0 + n) // 16]))
 
-        w_bf, w_codes, w_plane = {}, {}, {}
+        w_bf = [sb.tile([P, PASSES, P, PACK], BF16, name=f"w_bf{b}", align_bytes=64) for b in range(BLOCKS)]
+        w_codes, w_plane = {}, {}
 
         def cast_w(b, z):
-            t = sb.tile([P, P, PACK], BF16, name=f"w_bf{b}_{z}", align_bytes=64)
-            nc.scalar.copy(t[:].rearrange("p (c i) t -> p c t i", i=4),
+            nc.scalar.copy(w_bf[b][:, z].rearrange("p (c i) t -> p c t i", i=4),
                            w_raw[z][:, :, b * P:(b + 1) * P].rearrange("p t (c i) -> p c t i", i=4))
-            w_bf[(b, z)] = t
 
-        def quantize_w(b, z):
-            codes = sb.tile([P, P], U32, name=f"w_codes{b}_{z}", align_bytes=64)
-            plane = sb.tile([P, P], U8, name=f"w_plane{b}_{z}", align_bytes=64)
+        def quantize_w(b, tag):
+            codes = sb.tile([P, PASSES * P], U32, name=f"w_codes{b}", tag=tag, align_bytes=64)
+            plane = sb.tile([P, PASSES * P], U8, name=f"w_plane{b}", align_bytes=64)
             nc.vector.quantize_mx(out=codes[:].bitcast(FP8X4), scales=plane[:],
-                                  in_=w_bf[(b, z)][:].rearrange("p m t -> p (m t)"))
-            w_codes[(b, z)], w_plane[(b, z)] = codes, plane
+                                  in_=w_bf[b][:].rearrange("p z m t -> p (z m t)"))
+            for z in range(PASSES):
+                w_codes[(b, z)], w_plane[(b, z)] = codes[:, z * P:(z + 1) * P], plane[:, z * P:(z + 1) * P]
 
         def mm(acc, b, z, j0, n):
-            nc.tensor.matmul_mx(out=acc, lhsT=w_codes[(b, z)][:].bitcast(FP8X4), lhsT_scale=w_plane[(b, z)][:],
+            nc.tensor.matmul_mx(out=acc, lhsT=w_codes[(b, z)].bitcast(FP8X4), lhsT_scale=w_plane[(b, z)],
                                 rhs=picked_cols(z, j0, n).bitcast(FP4X4), rhs_scale=x_plane[z][:, j0:j0 + n],
                                 start=(z == 0), stop=(z == PASSES - 1))
 
@@ -102,30 +106,25 @@ def tile_picked_lerp_gelu_p_kernel(tc, x_words, x_scales, w1, frac, offs, left, 
         cast_w(1, 0)
         cast_w(1, 1)
         gather_words(*pieces[0])
-        quantize_w(0, 0)
         gather_words(*pieces[1])
-        quantize_w(0, 1)
+        quantize_w(0, "w_codes0")
         gather_words(*pieces[2])
-        quantize_w(1, 0)
         gather_words(*pieces[3])
         gather_words(*pieces[4])
-        quantize_w(1, 1)
+        quantize_w(1, "word_win1")
 
         rest = sb.tile([P, V], F32, name="rest", align_bytes=64)
-        nc.scalar.activation(rest[:], frac_t[:], ACT.Copy, bias=1.0, scale=-1.0)
+        nc.vector.tensor_scalar(rest[:], frac_t[:], -1.0, 1.0, ALU.mult, ALU.add)
 
         y = [sb.tile([P, S], F32, name=f"y{b}", align_bytes=64) for b in range(BLOCKS)]
         bank = {}
-        for b in range(BLOCKS):
-            for h in range(2):
-                bank[(b, h)] = psum.tile([P, 512], F32, name=f"bank{b}_{h}")
-        tail = [psum.tile([P, 512], F32, name=f"tail{g}") for g in range(2)]
+        for h in range(2):
+            bank[(0, h)] = psum.tile([P, 512], F32, name=f"bank0_{h}", tag=f"bank{h}")
+        tail = [psum.tile([P, 512], F32, name=f"tail{g}", tag=f"bank{4 + g}") for g in range(2)]
 
         mm(bank[(0, 0)][:], 0, 0, 0, 512)
         for g in range(2):
             mm(tail[g][:, 0:P], 0, 0, 768 + g * P, P)
-        mm(bank[(1, 0)][:], 1, 0, 0, 512)
-        mm(bank[(1, 1)][:], 1, 0, 512, 512)
         mm(bank[(0, 0)][:], 0, 1, 0, 512)
         nc.scalar.activation(y[0][:, 0:512], bank[(0, 0)][:], ACT.Gelu_apprx_tanh)
         for g in range(2):
@@ -136,17 +135,45 @@ def tile_picked_lerp_gelu_p_kernel(tc, x_words, x_scales, w1, frac, offs, left, 
             mm(tail[g][:, 0:P], 0, 1, 768 + g * P, P)
             nc.scalar.activation(y[0][:, 768 + g * P:768 + (g + 1) * P], tail[g][:, 0:P], ACT.Gelu_apprx_tanh)
         for h in range(2):
+            bank[(1, h)] = psum.tile([P, 512], F32, name=f"bank1_{h}", tag=f"bank{h}")
+            mm(bank[(1, h)][:], 1, 0, h * 512, 512)
             mm(bank[(1, h)][:], 1, 1, h * 512, 512)
             nc.scalar.activation(y[1][:, h * 512:(h + 1) * 512], bank[(1, h)][:], ACT.Gelu_apprx_tanh)
+
+        frac_ps = psum.tile([P, 4, P], F32, name="frac_ps", tag="bank4")
+        for c in range(4):
+            nc.tensor.transpose(frac_ps[:, c, :], frac_t[:, c * P:(c + 1) * P], ident[:])
+        frac_col = sb.tile([P, 4], F32, name="frac_col", align_bytes=64)
+        rest_col = sb.tile([P, 4], F32, name="rest_col", align_bytes=64)
+        nc.scalar.copy(frac_col[:], frac_ps[:, :, 0])
+        nc.scalar.activation(rest_col[:], frac_ps[:, :, 0], ACT.Copy, bias=1.0, scale=-1.0)
 
         part_l = [sb.tile([P, V], F32, name=f"part_l{b}", align_bytes=64) for b in range(BLOCKS)]
         part_r = [sb.tile([P, V], F32, name=f"part_r{b}", align_bytes=64) for b in range(BLOCKS)]
         res = [sb.tile([P, V], F32, name=f"res{b}", align_bytes=64) for b in range(BLOCKS)]
-        nc.vector.tensor_tensor(part_l[0][:], y[0][:].indirect(left_t[:]), rest[:], ALU.mult)
-        nc.vector.tensor_tensor(part_r[0][:], y[0][:].indirect(right_t[:]), frac_t[:], ALU.mult)
+        nc.vector.tensor_copy(part_l[0][:], y[0][:].indirect(left_t[:]))
+        nc.vector.tensor_copy(part_r[0][:], y[0][:].indirect(right_t[:]))
+        turned_l = sb.tile([P, 4, P], F32, name="turned_l", align_bytes=64)
+        turned_r = sb.tile([P, 4, P], F32, name="turned_r", align_bytes=64)
+        l_ps = psum.tile([P, 4, P], F32, name="l_ps", tag="bank6")
+        r_ps = [psum.tile([P, 4, P], F32, name=f"r_ps{h}", tag=tag) for h, tag in enumerate(("bank7", "bank2"))]
+        sum_ps = [psum.tile([P, 4, P], F32, name=f"sum_ps{c}", tag=f"bank{b}") for c, b in enumerate((3, 5, 4, 0))]
+        for c in range(4):
+            nc.tensor.transpose(l_ps[:, c, :], part_l[0][:, c * P:(c + 1) * P], ident[:])
+        for c in range(4):
+            nc.scalar.activation(turned_l[:, c, :], l_ps[:, c, :], ACT.Copy, scale=rest_col[:, c:c + 1])
+        for c in range(4):
+            nc.tensor.transpose(r_ps[c // 2][:, c % 2, :], part_r[0][:, c * P:(c + 1) * P], ident[:])
+        for c in range(4):
+            nc.tensor.matmul(sum_ps[c][:, 0, :], lhsT=turned_l[:, c, :], rhs=ident[:], is_transpose=True, start=True, stop=False)
+        for c in range(4):
+            nc.scalar.activation(turned_r[:, c, :], r_ps[c // 2][:, c % 2, :], ACT.Copy, scale=frac_col[:, c:c + 1])
+        for c in range(4):
+            nc.tensor.matmul(sum_ps[c][:, 0, :], lhsT=turned_r[:, c, :], rhs=ident[:], is_transpose=True, start=False, stop=True)
+            nc.scalar.copy(res[0][:, c * P:(c + 1) * P], sum_ps[c][:, 0, :])
+            if c % 2 == 1:
+                nc.sync.dma_start(out=out[0:P, (c - 1) * P:(c + 1) * P], in_=res[0][:, (c - 1) * P:(c + 1) * P])
         nc.vector.tensor_tensor(part_l[1][:], y[1][:].indirect(left_t[:]), rest[:], ALU.mult)
-        nc.vector.tensor_tensor(res[0][:], part_l[0][:], part_r[0][:], ALU.add)
-        nc.sync.dma_start(out=out[0:P, :], in_=res[0][:])
         half = V // 2
         for h in range(2):
             c = slice(h * half, (h + 1) * half)

@@ -34,15 +34,14 @@ def tile_picked_lerp_gelu_p_kernel(tc, x_words, x_scales, w1, frac, offs, left, 
         right_t = lists.tile([P, V // 16], U16, name="right_t")
 
         scale_win = sb.tile([P, T], U8, name="scale_win", tag="scales_then_frac", align_bytes=64)
-        nc.scalar.dma_start(out=scale_win[0:32, :].bitcast(I32), in_=x_scales.rearrange("z q c -> (z q) c").bitcast(I32))
+        nc.scalar.dma_start(out=scale_win[96:128, :].bitcast(I32), in_=x_scales.rearrange("z q c -> (z q) c").bitcast(I32))
         nc.sync.dma_start(offs_t[:], offs)
         nc.sync.dma_start(left_t[:], left)
         nc.sync.dma_start(right_t[:], right)
-        nc.vector.memset(scale_win[32:64, :].bitcast(I32), 0)
-        nc.vector.memset(scale_win[64:128, :].bitcast(I32), 0)
+        nc.vector.memset(scale_win[0:96, :].bitcast(I32), 0)
 
         word_win = [sb.tile([P, T], U16, name=f"word_win{z}", tag=f"word_win{z}", align_bytes=64) for z in range(PASSES)]
-        w_raw = [sb.tile([P, PACK, N], F32, name=f"w_raw{z}", align_bytes=64) for z in range(PASSES)]
+        w_raw = [sb.tile([P, PACK, N], F32, name=f"w_raw{z}", tag=f"w_raw{z}", align_bytes=64) for z in range(PASSES)]
         nc.sync.dma_start(out=word_win[0][:].bitcast(I32), in_=x_words[0].bitcast(I32))
         for z in range(PASSES):
             nc.sync.dma_start(out=w_raw[z][:], in_=w1[z * 512:(z + 1) * 512, :].rearrange("(p j) m -> p j m", j=PACK))
@@ -66,7 +65,7 @@ def tile_picked_lerp_gelu_p_kernel(tc, x_words, x_scales, w1, frac, offs, left, 
             queue = nc.scalar if z == 0 else nc.sync
             for r in range(4):
                 queue.dma_start(out=x_plane[z][r:P:32, :].bitcast(I32),
-                                in_=picked_scales[16 * z + r:16 * z + 16:4, :].bitcast(I32))
+                                in_=picked_scales[96 + 16 * z + r:96 + 16 * z + 16:4, :].bitcast(I32))
 
         frac_t = sb.tile([P, V], F32, name="frac_t", tag="scales_then_frac", align_bytes=64)
         nc.sync.dma_start(out=frac_t[:], in_=frac)
@@ -140,13 +139,11 @@ def tile_picked_lerp_gelu_p_kernel(tc, x_words, x_scales, w1, frac, offs, left, 
             mm(bank[(1, h)][:], 1, 1, h * 512, 512)
             nc.scalar.activation(y[1][:, h * 512:(h + 1) * 512], bank[(1, h)][:], ACT.Gelu_apprx_tanh)
 
-        frac_ps = psum.tile([P, 4, P], F32, name="frac_ps", tag="bank4")
-        for c in range(4):
-            nc.tensor.transpose(frac_ps[:, c, :], frac_t[:, c * P:(c + 1) * P], ident[:])
-        frac_col = sb.tile([P, 4], F32, name="frac_col", align_bytes=64)
+        frac_col = sb.tile([P, 4], F32, name="frac_col", tag="w_raw0", align_bytes=64)
         rest_col = sb.tile([P, 4], F32, name="rest_col", align_bytes=64)
-        nc.scalar.copy(frac_col[:], frac_ps[:, :, 0])
-        nc.scalar.activation(rest_col[:], frac_ps[:, :, 0], ACT.Copy, bias=1.0, scale=-1.0)
+        with nc.allow_non_contiguous_dma(reason="one value a partition and chunk"):
+            nc.sync.dma_start(out=frac_col[:], in_=frac[0].rearrange("(c p) -> p c", p=P))
+        nc.gpsimd.tensor_scalar(rest_col[:], frac_col[:], -1.0, 1.0, ALU.mult, ALU.add)
 
         part_l = [sb.tile([P, V], F32, name=f"part_l{b}", align_bytes=64) for b in range(BLOCKS)]
         part_r = [sb.tile([P, V], F32, name=f"part_r{b}", align_bytes=64) for b in range(BLOCKS)]
@@ -172,7 +169,7 @@ def tile_picked_lerp_gelu_p_kernel(tc, x_words, x_scales, w1, frac, offs, left, 
             nc.tensor.matmul(sum_ps[c][:, 0, :], lhsT=turned_r[:, c, :], rhs=ident[:], is_transpose=True, start=False, stop=True)
             nc.scalar.copy(res[0][:, c * P:(c + 1) * P], sum_ps[c][:, 0, :])
             if c % 2 == 1:
-                nc.sync.dma_start(out=out[0:P, (c - 1) * P:(c + 1) * P], in_=res[0][:, (c - 1) * P:(c + 1) * P])
+                nc.scalar.dma_start(out=out[0:P, (c - 1) * P:(c + 1) * P], in_=res[0][:, (c - 1) * P:(c + 1) * P])
         nc.vector.tensor_tensor(part_l[1][:], y[1][:].indirect(left_t[:]), rest[:], ALU.mult)
         half = V // 2
         for h in range(2):

@@ -50,11 +50,6 @@ def tile_picked_lerp_gelu_p_kernel(tc, x_words, x_scales, w1, frac, offs, left, 
         ident = sb.tile([P, P], F32, name="ident", align_bytes=64)
         make_identity(nc, ident[:])
 
-        warm = sb.tile([P, 8], F32, name="warm")
-        warm_out = sb.tile([P, 8], F32, name="warm_out")
-        nc.vector.memset(warm[:], 0.0)
-        nc.scalar.activation(warm_out[:], warm[:], ACT.Gelu_apprx_tanh)
-
         x_plane = [sb.tile([P, S], U8, name=f"x_plane{z}", align_bytes=64) for z in range(PASSES)]
         for z in range(PASSES):
             nc.vector.memset(x_plane[z][:].bitcast(I32), 0)
@@ -62,25 +57,25 @@ def tile_picked_lerp_gelu_p_kernel(tc, x_words, x_scales, w1, frac, offs, left, 
         picked_scales = sb.tile([P, S], U8, name="picked_scales", align_bytes=64)
         nc.vector.tensor_copy(picked_scales[:], scale_win[:].indirect(offs_t[:]))
         for z in range(PASSES):
-            queue = nc.scalar if z == 0 else nc.sync
             for r in range(4):
-                queue.dma_start(out=x_plane[z][r:P:32, :].bitcast(I32),
-                                in_=picked_scales[96 + 16 * z + r:96 + 16 * z + 16:4, :].bitcast(I32))
+                nc.sync.dma_start(out=x_plane[z][r:P:32, :].bitcast(I32),
+                                  in_=picked_scales[96 + 16 * z + r:96 + 16 * z + 16:4, :].bitcast(I32))
 
         frac_t = sb.tile([P, V], F32, name="frac_t", tag="scales_then_frac", align_bytes=64)
         nc.sync.dma_start(out=frac_t[:], in_=frac)
 
         pieces = [(0, 0, 512), (0, 512, 512), (1, 0, 512), (1, 512, 256), (1, 768, 256)]
-        picked = {(z, h): sb.tile([P, 512], U16, name=f"picked{z}_{h}", align_bytes=64)
-                  for z in range(PASSES) for h in range(2)}
+        picked = {}
 
         def picked_cols(z, j0, n):
-            return picked[(z, j0 // 512)][:, j0 % 512:j0 % 512 + n]
+            return picked[z][:, j0:j0 + n]
 
         def gather_words(z, j0, n):
+            if j0 == 0:
+                picked[z] = sb.tile([P, S], U16, name=f"picked{z}", tag="w_bf0" if z == 1 else "picked0", align_bytes=64)
             nc.vector.tensor_copy(picked_cols(z, j0, n), word_win[z][:].indirect(offs_t[:, j0 // 16:(j0 + n) // 16]))
 
-        w_bf = [sb.tile([P, PASSES, P, PACK], BF16, name=f"w_bf{b}", align_bytes=64) for b in range(BLOCKS)]
+        w_bf = [sb.tile([P, PASSES, P, PACK], BF16, name=f"w_bf{b}", tag=f"w_bf{b}", align_bytes=64) for b in range(BLOCKS)]
         w_codes, w_plane = {}, {}
 
         def cast_w(b, z):
@@ -133,11 +128,13 @@ def tile_picked_lerp_gelu_p_kernel(tc, x_words, x_scales, w1, frac, offs, left, 
         for g in range(2):
             mm(tail[g][:, 0:P], 0, 1, 768 + g * P, P)
             nc.scalar.activation(y[0][:, 768 + g * P:768 + (g + 1) * P], tail[g][:, 0:P], ACT.Gelu_apprx_tanh)
-        for h in range(2):
-            bank[(1, h)] = psum.tile([P, 512], F32, name=f"bank1_{h}", tag=f"bank{h}")
-            mm(bank[(1, h)][:], 1, 0, h * 512, 512)
-            mm(bank[(1, h)][:], 1, 1, h * 512, 512)
-            nc.scalar.activation(y[1][:, h * 512:(h + 1) * 512], bank[(1, h)][:], ACT.Gelu_apprx_tanh)
+        for j0, n, tag in ((0, 512, "bank0"), (512, 256, "bank1"), (768, 128, "bank4"), (896, 128, "bank5")):
+            acc = psum.tile([P, 512], F32, name=f"acc1_{j0}", tag=tag)
+            width = 512 if n == 512 else P
+            for g0 in range(0, n, width):
+                for z in range(PASSES):
+                    mm(acc[:, g0:g0 + width], 1, z, j0 + g0, width)
+            nc.scalar.activation(y[1][:, j0:j0 + n], acc[:, 0:n], ACT.Gelu_apprx_tanh)
 
         frac_col = sb.tile([P, 4], F32, name="frac_col", tag="w_raw0", align_bytes=64)
         rest_col = sb.tile([P, 4], F32, name="rest_col", align_bytes=64)
@@ -154,7 +151,7 @@ def tile_picked_lerp_gelu_p_kernel(tc, x_words, x_scales, w1, frac, offs, left, 
         turned_r = sb.tile([P, 4, P], F32, name="turned_r", align_bytes=64)
         l_ps = psum.tile([P, 4, P], F32, name="l_ps", tag="bank6")
         r_ps = [psum.tile([P, 4, P], F32, name=f"r_ps{h}", tag=tag) for h, tag in enumerate(("bank7", "bank2"))]
-        sum_ps = [psum.tile([P, 4, P], F32, name=f"sum_ps{c}", tag=f"bank{b}") for c, b in enumerate((3, 5, 4, 0))]
+        sum_ps = [psum.tile([P, 4, P], F32, name=f"sum_ps{c}", tag=f"bank{b}") for c, b in enumerate((3, 0, 1, 4))]
         for c in range(4):
             nc.tensor.transpose(l_ps[:, c, :], part_l[0][:, c * P:(c + 1) * P], ident[:])
         for c in range(4):

@@ -6,9 +6,21 @@ from concourse.masks import make_identity
 K, T, S, V, N = 1024, 2048, 1024, 512, 256
 P = 128
 PACK = 4
-PASSES = K // (P * PACK)
-BLOCKS = N // P
+K_PASS = P * PACK
+PASSES = K // K_PASS
+ROW_BLOCKS = N // P
+STRIPE = 16
+QUADRANT = 32
+QUADRANT_ROWS = 4
+PASS_ROWS = K_PASS // 32
+SCALE_ROW0 = P - PASSES * PASS_ROWS
+RUN = 4
+BANK = 512
+CHUNKS = V // P
 FLOPS = 2 * K * N * S
+
+WIDE, NARROW = 512, 256
+TAIL0 = WIDE + NARROW
 
 F32 = mybir.dt.float32
 BF16 = mybir.dt.bfloat16
@@ -18,8 +30,10 @@ U16 = mybir.dt.uint16
 U8 = mybir.dt.uint8
 FP8X4 = mybir.dt.float8_e4m3fn_x4
 FP4X4 = mybir.dt.float4_e2m1fn_x4
-ACT = mybir.ActivationFunctionType
-ALU = mybir.AluOpType
+GELU = mybir.ActivationFunctionType.Gelu_apprx_tanh
+COPY = mybir.ActivationFunctionType.Copy
+MULT = mybir.AluOpType.mult
+ADD = mybir.AluOpType.add
 
 
 def tile_picked_lerp_gelu_p_kernel(tc, x_words, x_scales, w1, frac, offs, left, right, out):
@@ -29,150 +43,152 @@ def tile_picked_lerp_gelu_p_kernel(tc, x_words, x_scales, w1, frac, offs, left, 
         sb = ctx.enter_context(tc.tile_pool(name="sb", bufs=1))
         psum = ctx.enter_context(tc.psum_pool(name="psum", bufs=1))
 
-        offs_t = lists.tile([P, S // 16], U16, name="offs_t")
-        left_t = lists.tile([P, V // 16], U16, name="left_t")
-        right_t = lists.tile([P, V // 16], U16, name="right_t")
+        offs_t = lists.tile([P, S // STRIPE], U16, name="offs_t")
+        left_t = lists.tile([P, V // STRIPE], U16, name="left_t")
+        right_t = lists.tile([P, V // STRIPE], U16, name="right_t")
 
         scale_win = sb.tile([P, T], U8, name="scale_win", tag="scales_then_frac", align_bytes=64)
-        nc.scalar.dma_start(out=scale_win[96:128, :].bitcast(I32), in_=x_scales.rearrange("z q c -> (z q) c").bitcast(I32))
+        nc.scalar.dma_start(out=scale_win[SCALE_ROW0:P, :].bitcast(I32),
+                            in_=x_scales.rearrange("z q c -> (z q) c").bitcast(I32))
         nc.sync.dma_start(offs_t[:], offs)
         nc.sync.dma_start(left_t[:], left)
         nc.sync.dma_start(right_t[:], right)
-        nc.vector.memset(scale_win[0:96, :].bitcast(I32), 0)
+        nc.vector.memset(scale_win[0:SCALE_ROW0, :].bitcast(I32), 0)
 
         word_win = [sb.tile([P, T], U16, name=f"word_win{z}", tag=f"word_win{z}", align_bytes=64) for z in range(PASSES)]
-        w_raw = [sb.tile([P, PACK, N], F32, name=f"w_raw{z}", tag=f"w_raw{z}", align_bytes=64) for z in range(PASSES)]
+        w_raw = [sb.tile([P, PACK, N], F32, name=f"w_raw{z}", align_bytes=64) for z in range(PASSES)]
         nc.sync.dma_start(out=word_win[0][:].bitcast(I32), in_=x_words[0].bitcast(I32))
         for z in range(PASSES):
-            nc.sync.dma_start(out=w_raw[z][:], in_=w1[z * 512:(z + 1) * 512, :].rearrange("(p j) m -> p j m", j=PACK))
+            nc.sync.dma_start(out=w_raw[z][:], in_=w1[z * K_PASS:(z + 1) * K_PASS, :].rearrange("(p t) m -> p t m", t=PACK))
         nc.sync.dma_start(out=word_win[1][:].bitcast(I32), in_=x_words[1].bitcast(I32))
 
         ident = sb.tile([P, P], F32, name="ident", align_bytes=64)
         make_identity(nc, ident[:])
 
+        warm = sb.tile([P, 8], F32, name="warm")
+        warm_out = sb.tile([P, 8], F32, name="warm_out")
+        nc.vector.memset(warm[:], 0.0)
+        nc.scalar.activation(warm_out[:], warm[:], GELU)
+
         x_plane = [sb.tile([P, S], U8, name=f"x_plane{z}", align_bytes=64) for z in range(PASSES)]
         for z in range(PASSES):
             nc.vector.memset(x_plane[z][:].bitcast(I32), 0)
 
-        picked_scales = sb.tile([P, S], U8, name="picked_scales", align_bytes=64)
+        picked_scales = sb.tile([P, S], U8, name="picked_scales", tag="picked_scales", align_bytes=64)
         nc.vector.tensor_copy(picked_scales[:], scale_win[:].indirect(offs_t[:]))
         for z in range(PASSES):
-            for r in range(4):
-                nc.sync.dma_start(out=x_plane[z][r:P:32, :].bitcast(I32),
-                                  in_=picked_scales[96 + 16 * z + r:96 + 16 * z + 16:4, :].bitcast(I32))
+            row0 = SCALE_ROW0 + PASS_ROWS * z
+            for r in range(QUADRANT_ROWS):
+                nc.sync.dma_start(out=x_plane[z][r:P:QUADRANT, :].bitcast(I32),
+                                  in_=picked_scales[row0 + r:row0 + PASS_ROWS:QUADRANT_ROWS, :].bitcast(I32))
 
         frac_t = sb.tile([P, V], F32, name="frac_t", tag="scales_then_frac", align_bytes=64)
         nc.sync.dma_start(out=frac_t[:], in_=frac)
 
-        pieces = [(0, 0, 512), (0, 512, 512), (1, 0, 512), (1, 512, 256), (1, 768, 256)]
-        picked = {}
+        w_bf = [sb.tile([P, PASSES, P, PACK], BF16, name=f"w_bf{b}", tag=f"w_bf{b}", align_bytes=64) for b in range(ROW_BLOCKS)]
+        for b in range(ROW_BLOCKS):
+            for z in range(PASSES):
+                nc.scalar.copy(w_bf[b][:, z].rearrange("p (c i) t -> p c t i", i=RUN),
+                               w_raw[z][:, :, b * P:(b + 1) * P].rearrange("p t (c i) -> p c t i", i=RUN))
 
-        def picked_cols(z, j0, n):
-            return picked[z][:, j0:j0 + n]
+        picked, w_codes, w_plane = {}, {}, {}
 
         def gather_words(z, j0, n):
-            if j0 == 0:
-                picked[z] = sb.tile([P, S], U16, name=f"picked{z}", tag="w_bf0" if z == 1 else "picked0", align_bytes=64)
-            nc.vector.tensor_copy(picked_cols(z, j0, n), word_win[z][:].indirect(offs_t[:, j0 // 16:(j0 + n) // 16]))
-
-        w_bf = [sb.tile([P, PASSES, P, PACK], BF16, name=f"w_bf{b}", tag=f"w_bf{b}", align_bytes=64) for b in range(BLOCKS)]
-        w_codes, w_plane = {}, {}
-
-        def cast_w(b, z):
-            nc.scalar.copy(w_bf[b][:, z].rearrange("p (c i) t -> p c t i", i=4),
-                           w_raw[z][:, :, b * P:(b + 1) * P].rearrange("p t (c i) -> p c t i", i=4))
+            nc.vector.tensor_copy(picked[z][:, j0:j0 + n],
+                                  word_win[z][:].indirect(offs_t[:, j0 // STRIPE:(j0 + n) // STRIPE]))
 
         def quantize_w(b, tag):
-            codes = sb.tile([P, PASSES * P], U32, name=f"w_codes{b}", tag=tag, align_bytes=64)
-            plane = sb.tile([P, PASSES * P], U8, name=f"w_plane{b}", align_bytes=64)
-            nc.vector.quantize_mx(out=codes[:].bitcast(FP8X4), scales=plane[:],
+            w_codes[b] = sb.tile([P, PASSES * P], U32, name=f"w_codes{b}", tag=tag, align_bytes=64)
+            w_plane[b] = sb.tile([P, PASSES * P], U8, name=f"w_plane{b}", align_bytes=64)
+            nc.vector.quantize_mx(out=w_codes[b][:].bitcast(FP8X4), scales=w_plane[b][:],
                                   in_=w_bf[b][:].rearrange("p z m t -> p (z m t)"))
-            for z in range(PASSES):
-                w_codes[(b, z)], w_plane[(b, z)] = codes[:, z * P:(z + 1) * P], plane[:, z * P:(z + 1) * P]
 
-        def mm(acc, b, z, j0, n):
-            nc.tensor.matmul_mx(out=acc, lhsT=w_codes[(b, z)].bitcast(FP8X4), lhsT_scale=w_plane[(b, z)],
-                                rhs=picked_cols(z, j0, n).bitcast(FP4X4), rhs_scale=x_plane[z][:, j0:j0 + n],
+        def product(acc, b, z, j0, n):
+            nc.tensor.matmul_mx(out=acc,
+                                lhsT=w_codes[b][:, z * P:(z + 1) * P].bitcast(FP8X4),
+                                lhsT_scale=w_plane[b][:, z * P:(z + 1) * P],
+                                rhs=picked[z][:, j0:j0 + n].bitcast(FP4X4),
+                                rhs_scale=x_plane[z][:, j0:j0 + n],
                                 start=(z == 0), stop=(z == PASSES - 1))
 
-        cast_w(0, 0)
-        cast_w(0, 1)
-        cast_w(1, 0)
-        cast_w(1, 1)
-        gather_words(*pieces[0])
-        gather_words(*pieces[1])
+        picked[0] = sb.tile([P, S], U16, name="picked0", tag="picked0", align_bytes=64)
+        gather_words(0, 0, WIDE)
+        gather_words(0, WIDE, S - WIDE)
         quantize_w(0, "w_codes0")
-        gather_words(*pieces[2])
-        gather_words(*pieces[3])
-        gather_words(*pieces[4])
+        picked[1] = sb.tile([P, S], U16, name="picked1", tag="w_bf0", align_bytes=64)
+        gather_words(1, 0, WIDE)
+        gather_words(1, WIDE, NARROW)
+        gather_words(1, TAIL0, S - TAIL0)
         quantize_w(1, "word_win1")
 
         rest = sb.tile([P, V], F32, name="rest", align_bytes=64)
-        nc.vector.tensor_scalar(rest[:], frac_t[:], -1.0, 1.0, ALU.mult, ALU.add)
+        nc.vector.tensor_scalar(rest[:], frac_t[:], -1.0, 1.0, MULT, ADD)
 
-        y = [sb.tile([P, S], F32, name=f"y{b}", align_bytes=64) for b in range(BLOCKS)]
-        bank = {}
-        for h in range(2):
-            bank[(0, h)] = psum.tile([P, 512], F32, name=f"bank0_{h}", tag=f"bank{h}")
-        tail = [psum.tile([P, 512], F32, name=f"tail{g}", tag=f"bank{4 + g}") for g in range(2)]
+        y = [sb.tile([P, S], F32, name=f"y{b}", align_bytes=64) for b in range(ROW_BLOCKS)]
+        acc_wide = psum.tile([P, BANK], F32, name="acc_wide", tag="bank0")
+        acc_narrow = psum.tile([P, BANK], F32, name="acc_narrow", tag="bank1")
+        acc_tail = [psum.tile([P, BANK], F32, name=f"acc_tail{g}", tag=f"bank{4 + g}") for g in range(2)]
 
-        mm(bank[(0, 0)][:], 0, 0, 0, 512)
+        product(acc_wide[:], 0, 0, 0, WIDE)
         for g in range(2):
-            mm(tail[g][:, 0:P], 0, 0, 768 + g * P, P)
-        mm(bank[(0, 0)][:], 0, 1, 0, 512)
-        nc.scalar.activation(y[0][:, 0:512], bank[(0, 0)][:], ACT.Gelu_apprx_tanh)
-        for g in range(2):
+            product(acc_tail[g][:, 0:P], 0, 0, TAIL0 + g * P, P)
+        product(acc_wide[:], 0, 1, 0, WIDE)
+        nc.scalar.activation(y[0][:, 0:WIDE], acc_wide[:], GELU)
+        for g0 in range(0, NARROW, P):
             for z in range(PASSES):
-                mm(bank[(0, 1)][:, g * P:(g + 1) * P], 0, z, 512 + g * P, P)
-        nc.scalar.activation(y[0][:, 512:768], bank[(0, 1)][:, 0:256], ACT.Gelu_apprx_tanh)
+                product(acc_narrow[:, g0:g0 + P], 0, z, WIDE + g0, P)
+        nc.scalar.activation(y[0][:, WIDE:TAIL0], acc_narrow[:, 0:NARROW], GELU)
         for g in range(2):
-            mm(tail[g][:, 0:P], 0, 1, 768 + g * P, P)
-            nc.scalar.activation(y[0][:, 768 + g * P:768 + (g + 1) * P], tail[g][:, 0:P], ACT.Gelu_apprx_tanh)
-        for j0, n, tag in ((0, 512, "bank0"), (512, 256, "bank1"), (768, 128, "bank4"), (896, 128, "bank5")):
-            acc = psum.tile([P, 512], F32, name=f"acc1_{j0}", tag=tag)
-            width = 512 if n == 512 else P
+            product(acc_tail[g][:, 0:P], 0, 1, TAIL0 + g * P, P)
+            nc.scalar.activation(y[0][:, TAIL0 + g * P:TAIL0 + (g + 1) * P], acc_tail[g][:, 0:P], GELU)
+
+        for j0, n, tag in ((0, WIDE, "bank0"), (WIDE, NARROW, "bank1"), (TAIL0, P, "bank4"), (TAIL0 + P, P, "bank5")):
+            acc = psum.tile([P, BANK], F32, name=f"acc1_{j0}", tag=tag)
+            width = WIDE if n == WIDE else P
             for g0 in range(0, n, width):
                 for z in range(PASSES):
-                    mm(acc[:, g0:g0 + width], 1, z, j0 + g0, width)
-            nc.scalar.activation(y[1][:, j0:j0 + n], acc[:, 0:n], ACT.Gelu_apprx_tanh)
+                    product(acc[:, g0:g0 + width], 1, z, j0 + g0, width)
+            nc.scalar.activation(y[1][:, j0:j0 + n], acc[:, 0:n], GELU)
 
-        frac_col = sb.tile([P, 4], F32, name="frac_col", tag="w_raw0", align_bytes=64)
-        rest_col = sb.tile([P, 4], F32, name="rest_col", align_bytes=64)
+        frac_col = sb.tile([P, CHUNKS], F32, name="frac_col", tag="picked_scales", align_bytes=64)
+        rest_col = sb.tile([P, CHUNKS], F32, name="rest_col", align_bytes=64)
         with nc.allow_non_contiguous_dma(reason="one value a partition and chunk"):
             nc.sync.dma_start(out=frac_col[:], in_=frac[0].rearrange("(c p) -> p c", p=P))
-        nc.gpsimd.tensor_scalar(rest_col[:], frac_col[:], -1.0, 1.0, ALU.mult, ALU.add)
+        nc.gpsimd.tensor_scalar(rest_col[:], frac_col[:], -1.0, 1.0, MULT, ADD)
 
-        part_l = [sb.tile([P, V], F32, name=f"part_l{b}", align_bytes=64) for b in range(BLOCKS)]
-        part_r = [sb.tile([P, V], F32, name=f"part_r{b}", align_bytes=64) for b in range(BLOCKS)]
-        res = [sb.tile([P, V], F32, name=f"res{b}", align_bytes=64) for b in range(BLOCKS)]
+        part_l = [sb.tile([P, V], F32, name=f"part_l{b}", align_bytes=64) for b in range(ROW_BLOCKS)]
+        part_r = [sb.tile([P, V], F32, name=f"part_r{b}", align_bytes=64) for b in range(ROW_BLOCKS)]
+        res = [sb.tile([P, V], F32, name=f"res{b}", align_bytes=64) for b in range(ROW_BLOCKS)]
+
         nc.vector.tensor_copy(part_l[0][:], y[0][:].indirect(left_t[:]))
         nc.vector.tensor_copy(part_r[0][:], y[0][:].indirect(right_t[:]))
-        turned_l = sb.tile([P, 4, P], F32, name="turned_l", align_bytes=64)
-        turned_r = sb.tile([P, 4, P], F32, name="turned_r", align_bytes=64)
-        l_ps = psum.tile([P, 4, P], F32, name="l_ps", tag="bank6")
-        r_ps = [psum.tile([P, 4, P], F32, name=f"r_ps{h}", tag=tag) for h, tag in enumerate(("bank7", "bank2"))]
-        sum_ps = [psum.tile([P, 4, P], F32, name=f"sum_ps{c}", tag=f"bank{b}") for c, b in enumerate((3, 0, 1, 4))]
-        for c in range(4):
+        turned_l = sb.tile([P, CHUNKS, P], F32, name="turned_l", align_bytes=64)
+        turned_r = sb.tile([P, CHUNKS, P], F32, name="turned_r", align_bytes=64)
+        l_ps = psum.tile([P, CHUNKS, P], F32, name="l_ps", tag="bank6")
+        r_ps = [psum.tile([P, CHUNKS, P], F32, name=f"r_ps{h}", tag=tag) for h, tag in enumerate(("bank7", "bank2"))]
+        sum_ps = [psum.tile([P, CHUNKS, P], F32, name=f"sum_ps{c}", tag=tag)
+                  for c, tag in enumerate(("bank3", "bank0", "bank1", "bank4"))]
+        for c in range(CHUNKS):
             nc.tensor.transpose(l_ps[:, c, :], part_l[0][:, c * P:(c + 1) * P], ident[:])
-        for c in range(4):
-            nc.scalar.activation(turned_l[:, c, :], l_ps[:, c, :], ACT.Copy, scale=rest_col[:, c:c + 1])
-        for c in range(4):
+        for c in range(CHUNKS):
+            nc.scalar.activation(turned_l[:, c, :], l_ps[:, c, :], COPY, scale=rest_col[:, c:c + 1])
+        for c in range(CHUNKS):
             nc.tensor.transpose(r_ps[c // 2][:, c % 2, :], part_r[0][:, c * P:(c + 1) * P], ident[:])
-        for c in range(4):
+        for c in range(CHUNKS):
             nc.tensor.matmul(sum_ps[c][:, 0, :], lhsT=turned_l[:, c, :], rhs=ident[:], is_transpose=True, start=True, stop=False)
-        for c in range(4):
-            nc.scalar.activation(turned_r[:, c, :], r_ps[c // 2][:, c % 2, :], ACT.Copy, scale=frac_col[:, c:c + 1])
-        for c in range(4):
+        for c in range(CHUNKS):
+            nc.scalar.activation(turned_r[:, c, :], r_ps[c // 2][:, c % 2, :], COPY, scale=frac_col[:, c:c + 1])
+        for c in range(CHUNKS):
             nc.tensor.matmul(sum_ps[c][:, 0, :], lhsT=turned_r[:, c, :], rhs=ident[:], is_transpose=True, start=False, stop=True)
             nc.scalar.copy(res[0][:, c * P:(c + 1) * P], sum_ps[c][:, 0, :])
             if c % 2 == 1:
                 nc.scalar.dma_start(out=out[0:P, (c - 1) * P:(c + 1) * P], in_=res[0][:, (c - 1) * P:(c + 1) * P])
-        nc.vector.tensor_tensor(part_l[1][:], y[1][:].indirect(left_t[:]), rest[:], ALU.mult)
-        half = V // 2
-        for h in range(2):
-            c = slice(h * half, (h + 1) * half)
-            nc.vector.tensor_tensor(part_r[1][:, c], y[1][:].indirect(right_t[:, h * 16:(h + 1) * 16]), frac_t[:, c], ALU.mult)
-        for h in range(2):
-            c = slice(h * half, (h + 1) * half)
-            nc.vector.tensor_tensor(res[1][:, c], part_l[1][:, c], part_r[1][:, c], ALU.add)
-            nc.sync.dma_start(out=out[P:2 * P, c], in_=res[1][:, c])
+
+        nc.vector.tensor_tensor(part_l[1][:], y[1][:].indirect(left_t[:]), rest[:], MULT)
+        halves = [slice(0, V // 2), slice(V // 2, V)]
+        for cols in halves:
+            entries = right_t[:, cols.start // STRIPE:cols.stop // STRIPE]
+            nc.vector.tensor_tensor(part_r[1][:, cols], y[1][:].indirect(entries), frac_t[:, cols], MULT)
+        for cols in halves:
+            nc.vector.tensor_tensor(res[1][:, cols], part_l[1][:, cols], part_r[1][:, cols], ADD)
+            nc.sync.dma_start(out=out[P:2 * P, cols], in_=res[1][:, cols])

@@ -1,7 +1,6 @@
 from contextlib import ExitStack
 
 import concourse.mybir as mybir
-from concourse.masks import make_identity
 
 K, T, S, V, N = 1024, 2048, 1024, 512, 256
 P = 128
@@ -16,11 +15,10 @@ PASS_ROWS = K_PASS // 32
 SCALE_ROW0 = P - PASSES * PASS_ROWS
 RUN = 4
 BANK = 512
-CHUNKS = V // P
+HALF = V // 2
 FLOPS = 2 * K * N * S
 
-WIDE, NARROW = 512, 256
-TAIL0 = WIDE + NARROW
+GROUPS = ((0, 512), (512, 256), (768, 256))
 
 F32 = mybir.dt.float32
 BF16 = mybir.dt.bfloat16
@@ -41,6 +39,7 @@ def tile_picked_lerp_gelu_p_kernel(tc, x_words, x_scales, w1, frac, offs, left, 
     with ExitStack() as ctx:
         lists = ctx.enter_context(tc.tile_pool(name="lists", bufs=1))
         sb = ctx.enter_context(tc.tile_pool(name="sb", bufs=1))
+        late = ctx.enter_context(tc.tile_pool(name="late", bufs=1))
         psum = ctx.enter_context(tc.psum_pool(name="psum", bufs=1))
 
         offs_t = lists.tile([P, S // STRIPE], U16, name="offs_t")
@@ -55,15 +54,13 @@ def tile_picked_lerp_gelu_p_kernel(tc, x_words, x_scales, w1, frac, offs, left, 
         nc.sync.dma_start(right_t[:], right)
         nc.vector.memset(scale_win[0:SCALE_ROW0, :].bitcast(I32), 0)
 
-        word_win = [sb.tile([P, T], U16, name=f"word_win{z}", tag=f"word_win{z}", align_bytes=64) for z in range(PASSES)]
+        word_win = [sb.tile([P, T], U16, name="word_win0", align_bytes=64),
+                    late.tile([P, T], U16, name="word_win1", offset=0, align_bytes=64)]
         w_raw = [sb.tile([P, PACK, N], F32, name=f"w_raw{z}", align_bytes=64) for z in range(PASSES)]
         nc.sync.dma_start(out=word_win[0][:].bitcast(I32), in_=x_words[0].bitcast(I32))
         for z in range(PASSES):
             nc.sync.dma_start(out=w_raw[z][:], in_=w1[z * K_PASS:(z + 1) * K_PASS, :].rearrange("(p t) m -> p t m", t=PACK))
         nc.sync.dma_start(out=word_win[1][:].bitcast(I32), in_=x_words[1].bitcast(I32))
-
-        ident = sb.tile([P, P], F32, name="ident", align_bytes=64)
-        make_identity(nc, ident[:])
 
         warm = sb.tile([P, 8], F32, name="warm")
         warm_out = sb.tile([P, 8], F32, name="warm_out")
@@ -74,7 +71,7 @@ def tile_picked_lerp_gelu_p_kernel(tc, x_words, x_scales, w1, frac, offs, left, 
         for z in range(PASSES):
             nc.vector.memset(x_plane[z][:].bitcast(I32), 0)
 
-        picked_scales = sb.tile([P, S], U8, name="picked_scales", tag="picked_scales", align_bytes=64)
+        picked_scales = sb.tile([P, S], U8, name="picked_scales", align_bytes=64)
         nc.vector.tensor_copy(picked_scales[:], scale_win[:].indirect(offs_t[:]))
         for z in range(PASSES):
             row0 = SCALE_ROW0 + PASS_ROWS * z
@@ -85,110 +82,85 @@ def tile_picked_lerp_gelu_p_kernel(tc, x_words, x_scales, w1, frac, offs, left, 
         frac_t = sb.tile([P, V], F32, name="frac_t", tag="scales_then_frac", align_bytes=64)
         nc.sync.dma_start(out=frac_t[:], in_=frac)
 
-        w_bf = [sb.tile([P, PASSES, P, PACK], BF16, name=f"w_bf{b}", tag=f"w_bf{b}", align_bytes=64) for b in range(ROW_BLOCKS)]
-        for b in range(ROW_BLOCKS):
-            for z in range(PASSES):
-                nc.scalar.copy(w_bf[b][:, z].rearrange("p (c i) t -> p c t i", i=RUN),
-                               w_raw[z][:, :, b * P:(b + 1) * P].rearrange("p t (c i) -> p c t i", i=RUN))
+        parts = ((0, 0, N), (1, 0, P), (1, P, P))
+        w_bf, w_codes, w_plane, picked = {}, {}, {}, {}
+        for z, m0, m in parts:
+            w_bf[z, m0] = sb.tile([P, m, PACK], BF16, name=f"w_bf{z}_{m0}", tag=f"w_bf{z}_{m0}", align_bytes=64)
+            nc.scalar.copy(w_bf[z, m0][:].rearrange("p (c i) t -> p c t i", i=RUN),
+                           w_raw[z][:, :, m0:m0 + m].rearrange("p t (c i) -> p c t i", i=RUN))
 
-        picked, w_codes, w_plane = {}, {}, {}
+        def gather_words(z, j0, n, tag):
+            picked[z, j0] = sb.tile([P, n], U16, name=f"picked{z}_{j0}", tag=tag, align_bytes=64)
+            nc.vector.tensor_copy(picked[z, j0][:], word_win[z][:].indirect(offs_t[:, j0 // STRIPE:(j0 + n) // STRIPE]))
 
-        def gather_words(z, j0, n):
-            nc.vector.tensor_copy(picked[z][:, j0:j0 + n],
-                                  word_win[z][:].indirect(offs_t[:, j0 // STRIPE:(j0 + n) // STRIPE]))
+        def quantize_w(z, m0, m, codes):
+            plane = sb.tile([P, m], U8, name=f"w_plane{z}_{m0}", align_bytes=64)
+            nc.vector.quantize_mx(out=codes[:].bitcast(FP8X4), scales=plane[:],
+                                  in_=w_bf[z, m0][:].rearrange("p m t -> p (m t)"))
+            for b in range(m0 // P, (m0 + m) // P):
+                w_codes[z, b] = codes[:, b * P - m0:(b + 1) * P - m0]
+                w_plane[z, b] = plane[:, b * P - m0:(b + 1) * P - m0]
 
-        def quantize_w(b, tag):
-            w_codes[b] = sb.tile([P, PASSES * P], U32, name=f"w_codes{b}", tag=tag, align_bytes=64)
-            w_plane[b] = sb.tile([P, PASSES * P], U8, name=f"w_plane{b}", align_bytes=64)
-            nc.vector.quantize_mx(out=w_codes[b][:].bitcast(FP8X4), scales=w_plane[b][:],
-                                  in_=w_bf[b][:].rearrange("p z m t -> p (z m t)"))
-
-        def product(acc, b, z, j0, n):
-            nc.tensor.matmul_mx(out=acc,
-                                lhsT=w_codes[b][:, z * P:(z + 1) * P].bitcast(FP8X4),
-                                lhsT_scale=w_plane[b][:, z * P:(z + 1) * P],
-                                rhs=picked[z][:, j0:j0 + n].bitcast(FP4X4),
-                                rhs_scale=x_plane[z][:, j0:j0 + n],
-                                start=(z == 0), stop=(z == PASSES - 1))
-
-        picked[0] = sb.tile([P, S], U16, name="picked0", tag="picked0", align_bytes=64)
-        gather_words(0, 0, WIDE)
-        gather_words(0, WIDE, S - WIDE)
-        quantize_w(0, "w_codes0")
-        picked[1] = sb.tile([P, S], U16, name="picked1", tag="w_bf0", align_bytes=64)
-        gather_words(1, 0, WIDE)
-        gather_words(1, WIDE, NARROW)
-        gather_words(1, TAIL0, S - TAIL0)
-        quantize_w(1, "word_win1")
-
-        rest = sb.tile([P, V], F32, name="rest", align_bytes=64)
+        gather_words(0, 0, 512, "picked0_0")
+        gather_words(0, 512, 512, "picked0_512")
+        quantize_w(0, 0, N, sb.tile([P, N], U32, name="codes0", align_bytes=64))
+        gather_words(1, 0, 512, "w_bf0_0")
+        quantize_w(1, 0, P, sb.tile([P, P], U32, name="codes1_0", align_bytes=64))
+        gather_words(1, 512, 256, "w_bf1_0")
+        gather_words(1, 768, 256, "picked1_768")
+        quantize_w(1, P, P, late.tile([P, P], U32, name="codes1_1", offset=0, align_bytes=64))
+        rest = late.tile([P, V], F32, name="rest", offset=1024, align_bytes=64)
         nc.vector.tensor_scalar(rest[:], frac_t[:], -1.0, 1.0, MULT, ADD)
 
         y = [sb.tile([P, S], F32, name=f"y{b}", align_bytes=64) for b in range(ROW_BLOCKS)]
-        acc_wide = psum.tile([P, BANK], F32, name="acc_wide", tag="bank0")
-        acc_narrow = psum.tile([P, BANK], F32, name="acc_narrow", tag="bank1")
-        acc_tail = [psum.tile([P, BANK], F32, name=f"acc_tail{g}", tag=f"bank{4 + g}") for g in range(2)]
+        acc = {}
 
-        product(acc_wide[:], 0, 0, 0, WIDE)
-        for g in range(2):
-            product(acc_tail[g][:, 0:P], 0, 0, TAIL0 + g * P, P)
-        product(acc_wide[:], 0, 1, 0, WIDE)
-        nc.scalar.activation(y[0][:, 0:WIDE], acc_wide[:], GELU)
-        for g0 in range(0, NARROW, P):
-            for z in range(PASSES):
-                product(acc_narrow[:, g0:g0 + P], 0, z, WIDE + g0, P)
-        nc.scalar.activation(y[0][:, WIDE:TAIL0], acc_narrow[:, 0:NARROW], GELU)
-        for g in range(2):
-            product(acc_tail[g][:, 0:P], 0, 1, TAIL0 + g * P, P)
-            nc.scalar.activation(y[0][:, TAIL0 + g * P:TAIL0 + (g + 1) * P], acc_tail[g][:, 0:P], GELU)
+        def product(b, z, j0, n, bank=None):
+            if z == 0:
+                acc[b, j0] = psum.tile([P, BANK], F32, name=f"acc{b}_{j0}", tag=bank)
+            first = j0 // 512 * 512 if z == 0 else j0
+            nc.tensor.matmul_mx(out=acc[b, j0][:, 0:n],
+                                lhsT=w_codes[z, b].bitcast(FP8X4), lhsT_scale=w_plane[z, b],
+                                rhs=picked[z, first][:, j0 - first:j0 - first + n].bitcast(FP4X4),
+                                rhs_scale=x_plane[z][:, j0:j0 + n],
+                                start=(z == 0), stop=(z == PASSES - 1))
+            if z == PASSES - 1:
+                nc.scalar.activation(y[b][:, j0:j0 + n], acc[b, j0][:, 0:n], GELU)
 
-        for j0, n, tag in ((0, WIDE, "bank0"), (WIDE, NARROW, "bank1"), (TAIL0, P, "bank4"), (TAIL0 + P, P, "bank5")):
-            acc = psum.tile([P, BANK], F32, name=f"acc1_{j0}", tag=tag)
-            width = WIDE if n == WIDE else P
-            for g0 in range(0, n, width):
-                for z in range(PASSES):
-                    product(acc[:, g0:g0 + width], 1, z, j0 + g0, width)
-            nc.scalar.activation(y[1][:, j0:j0 + n], acc[:, 0:n], GELU)
+        for g, (j0, n) in enumerate(GROUPS):
+            product(0, 0, j0, n, f"bank{g}")
+        product(1, 0, *GROUPS[0], "bank3")
+        for j0, n in GROUPS:
+            product(0, 1, j0, n)
+        for g in (1, 2):
+            product(1, 0, *GROUPS[g], f"bank{g - 1}")
+        for j0, n in GROUPS:
+            product(1, 1, j0, n)
 
-        frac_col = sb.tile([P, CHUNKS], F32, name="frac_col", tag="picked_scales", align_bytes=64)
-        rest_col = sb.tile([P, CHUNKS], F32, name="rest_col", align_bytes=64)
-        with nc.allow_non_contiguous_dma(reason="one value a partition and chunk"):
-            nc.sync.dma_start(out=frac_col[:], in_=frac[0].rearrange("(c p) -> p c", p=P))
-        nc.gpsimd.tensor_scalar(rest_col[:], frac_col[:], -1.0, 1.0, MULT, ADD)
+        halves = [slice(0, HALF), slice(HALF, V)]
 
-        part_l = [sb.tile([P, V], F32, name=f"part_l{b}", align_bytes=64) for b in range(ROW_BLOCKS)]
-        part_r = [sb.tile([P, V], F32, name=f"part_r{b}", align_bytes=64) for b in range(ROW_BLOCKS)]
+        def entries(lst, cols):
+            return lst[:, cols.start // STRIPE:cols.stop // STRIPE]
+
+        lo_w = [sb.tile([P, V], F32, name=f"lo_w{b}", align_bytes=64) for b in range(ROW_BLOCKS)]
+        hi_w = [sb.tile([P, V], F32, name=f"hi_w{b}", align_bytes=64) for b in range(ROW_BLOCKS)]
         res = [sb.tile([P, V], F32, name=f"res{b}", align_bytes=64) for b in range(ROW_BLOCKS)]
+        lo = sb.tile([P, V], F32, name="lo", align_bytes=64)
+        hi = sb.tile([P, V], F32, name="hi", align_bytes=64)
 
-        nc.vector.tensor_copy(part_l[0][:], y[0][:].indirect(left_t[:]))
-        nc.vector.tensor_copy(part_r[0][:], y[0][:].indirect(right_t[:]))
-        turned_l = sb.tile([P, CHUNKS, P], F32, name="turned_l", align_bytes=64)
-        turned_r = sb.tile([P, CHUNKS, P], F32, name="turned_r", align_bytes=64)
-        l_ps = psum.tile([P, CHUNKS, P], F32, name="l_ps", tag="bank6")
-        r_ps = [psum.tile([P, CHUNKS, P], F32, name=f"r_ps{h}", tag=tag) for h, tag in enumerate(("bank7", "bank2"))]
-        sum_ps = [psum.tile([P, CHUNKS, P], F32, name=f"sum_ps{c}", tag=tag)
-                  for c, tag in enumerate(("bank3", "bank0", "bank1", "bank4"))]
-        for c in range(CHUNKS):
-            nc.tensor.transpose(l_ps[:, c, :], part_l[0][:, c * P:(c + 1) * P], ident[:])
-        for c in range(CHUNKS):
-            nc.scalar.activation(turned_l[:, c, :], l_ps[:, c, :], COPY, scale=rest_col[:, c:c + 1])
-        for c in range(CHUNKS):
-            nc.tensor.transpose(r_ps[c // 2][:, c % 2, :], part_r[0][:, c * P:(c + 1) * P], ident[:])
-        for c in range(CHUNKS):
-            nc.tensor.matmul(sum_ps[c][:, 0, :], lhsT=turned_l[:, c, :], rhs=ident[:], is_transpose=True, start=True, stop=False)
-        for c in range(CHUNKS):
-            nc.scalar.activation(turned_r[:, c, :], r_ps[c // 2][:, c % 2, :], COPY, scale=frac_col[:, c:c + 1])
-        for c in range(CHUNKS):
-            nc.tensor.matmul(sum_ps[c][:, 0, :], lhsT=turned_r[:, c, :], rhs=ident[:], is_transpose=True, start=False, stop=True)
-            nc.scalar.copy(res[0][:, c * P:(c + 1) * P], sum_ps[c][:, 0, :])
-            if c % 2 == 1:
-                nc.scalar.dma_start(out=out[0:P, (c - 1) * P:(c + 1) * P], in_=res[0][:, (c - 1) * P:(c + 1) * P])
+        nc.scalar.activation(lo[:], y[1][:].indirect(left_t[:]), COPY)
+        for cols in halves:
+            nc.scalar.activation(hi[:, cols], y[1][:].indirect(entries(right_t, cols)), COPY)
 
-        nc.vector.tensor_tensor(part_l[1][:], y[1][:].indirect(left_t[:]), rest[:], MULT)
-        halves = [slice(0, V // 2), slice(V // 2, V)]
+        nc.vector.tensor_tensor(lo_w[0][:], y[0][:].indirect(left_t[:]), rest[:], MULT)
         for cols in halves:
-            entries = right_t[:, cols.start // STRIPE:cols.stop // STRIPE]
-            nc.vector.tensor_tensor(part_r[1][:, cols], y[1][:].indirect(entries), frac_t[:, cols], MULT)
+            nc.vector.tensor_tensor(hi_w[0][:, cols], y[0][:].indirect(entries(right_t, cols)), frac_t[:, cols], MULT)
         for cols in halves:
-            nc.vector.tensor_tensor(res[1][:, cols], part_l[1][:, cols], part_r[1][:, cols], ADD)
+            nc.vector.tensor_tensor(res[0][:, cols], lo_w[0][:, cols], hi_w[0][:, cols], ADD)
+        nc.sync.dma_start(out=out[0:P, :], in_=res[0][:])
+        nc.vector.tensor_tensor(lo_w[1][:], lo[:], rest[:], MULT)
+        for cols in halves:
+            nc.vector.tensor_tensor(hi_w[1][:, cols], hi[:, cols], frac_t[:, cols], MULT)
+        for cols in halves:
+            nc.vector.tensor_tensor(res[1][:, cols], lo_w[1][:, cols], hi_w[1][:, cols], ADD)
             nc.sync.dma_start(out=out[P:2 * P, cols], in_=res[1][:, cols])

@@ -146,11 +146,10 @@ def tile_picked_lerp_gelu_p_kernel(tc, x_words, x_scales, w1, frac, offs, left, 
         hi_w = [sb.tile([P, V], F32, name=f"hi_w{b}", align_bytes=64) for b in range(ROW_BLOCKS)]
         res = [sb.tile([P, V], F32, name=f"res{b}", align_bytes=64) for b in range(ROW_BLOCKS)]
         lo = sb.tile([P, V], F32, name="lo", align_bytes=64)
-        hi = sb.tile([P, V], F32, name="hi", align_bytes=64)
+        hi = sb.tile([P, HALF], F32, name="hi", align_bytes=64)
 
         nc.scalar.activation(lo[:], y[1][:].indirect(left_t[:]), COPY)
-        for cols in halves:
-            nc.scalar.activation(hi[:, cols], y[1][:].indirect(entries(right_t, cols)), COPY)
+        nc.scalar.activation(hi[:], y[1][:].indirect(entries(right_t, halves[0])), COPY)
 
         nc.vector.tensor_tensor(lo_w[0][:], y[0][:].indirect(left_t[:]), rest[:], MULT)
         for cols in halves:
@@ -158,9 +157,9 @@ def tile_picked_lerp_gelu_p_kernel(tc, x_words, x_scales, w1, frac, offs, left, 
         for cols in halves:
             nc.vector.tensor_tensor(res[0][:, cols], lo_w[0][:, cols], hi_w[0][:, cols], ADD)
         nc.sync.dma_start(out=out[0:P, :], in_=res[0][:])
+        nc.vector.tensor_tensor(hi_w[1][:, halves[1]], y[1][:].indirect(entries(right_t, halves[1])), frac_t[:, halves[1]], MULT)
         nc.vector.tensor_tensor(lo_w[1][:], lo[:], rest[:], MULT)
-        for cols in halves:
-            nc.vector.tensor_tensor(hi_w[1][:, cols], hi[:, cols], frac_t[:, cols], MULT)
-        for cols in halves:
+        nc.vector.tensor_tensor(hi_w[1][:, halves[0]], hi[:], frac_t[:, halves[0]], MULT)
+        for cols in reversed(halves):
             nc.vector.tensor_tensor(res[1][:, cols], lo_w[1][:, cols], hi_w[1][:, cols], ADD)
             nc.sync.dma_start(out=out[P:2 * P, cols], in_=res[1][:, cols])

@@ -16,9 +16,11 @@ SCALE_ROW0 = P - PASSES * PASS_ROWS
 RUN = 4
 BANK = 512
 HALF = V // 2
+OWN = 128
 FLOPS = 2 * K * N * S
 
 GROUPS = ((0, 512), (512, 256), (768, 256))
+WIDE = ((0, 512), (512, 512))
 
 F32 = mybir.dt.float32
 BF16 = mybir.dt.bfloat16
@@ -82,33 +84,33 @@ def tile_picked_lerp_gelu_p_kernel(tc, x_words, x_scales, w1, frac, offs, left, 
         frac_t = sb.tile([P, V], F32, name="frac_t", tag="scales_then_frac", align_bytes=64)
         nc.sync.dma_start(out=frac_t[:], in_=frac)
 
-        parts = ((0, 0, N), (1, 0, P), (1, P, P))
-        w_bf, w_codes, w_plane, picked = {}, {}, {}, {}
-        for z, m0, m in parts:
-            w_bf[z, m0] = sb.tile([P, m, PACK], BF16, name=f"w_bf{z}_{m0}", tag=f"w_bf{z}_{m0}", align_bytes=64)
-            nc.scalar.copy(w_bf[z, m0][:].rearrange("p (c i) t -> p c t i", i=RUN),
-                           w_raw[z][:, :, m0:m0 + m].rearrange("p t (c i) -> p c t i", i=RUN))
+        w_bf = [sb.tile([P, PASSES, P, PACK], BF16, name=f"w_bf{b}", tag=f"w_bf{b}", align_bytes=64) for b in range(ROW_BLOCKS)]
+        for b in range(ROW_BLOCKS):
+            for z in range(PASSES):
+                nc.scalar.copy(w_bf[b][:, z].rearrange("p (c i) t -> p c t i", i=RUN),
+                               w_raw[z][:, :, b * P:(b + 1) * P].rearrange("p t (c i) -> p c t i", i=RUN))
 
-        def gather_words(z, j0, n, tag):
-            picked[z, j0] = sb.tile([P, n], U16, name=f"picked{z}_{j0}", tag=tag, align_bytes=64)
-            nc.vector.tensor_copy(picked[z, j0][:], word_win[z][:].indirect(offs_t[:, j0 // STRIPE:(j0 + n) // STRIPE]))
+        w_codes, w_plane = {}, {}
 
-        def quantize_w(z, m0, m, codes):
-            plane = sb.tile([P, m], U8, name=f"w_plane{z}_{m0}", align_bytes=64)
+        def gather_words(z, cuts, tag):
+            tile = sb.tile([P, S], U16, name=f"picked{z}", tag=tag, align_bytes=64)
+            for j0, n in cuts:
+                nc.vector.tensor_copy(tile[:, j0:j0 + n],
+                                      word_win[z][:].indirect(offs_t[:, j0 // STRIPE:(j0 + n) // STRIPE]))
+            return tile
+
+        def quantize_w(b, codes):
+            plane = sb.tile([P, PASSES * P], U8, name=f"w_plane{b}", align_bytes=64)
             nc.vector.quantize_mx(out=codes[:].bitcast(FP8X4), scales=plane[:],
-                                  in_=w_bf[z, m0][:].rearrange("p m t -> p (m t)"))
-            for b in range(m0 // P, (m0 + m) // P):
-                w_codes[z, b] = codes[:, b * P - m0:(b + 1) * P - m0]
-                w_plane[z, b] = plane[:, b * P - m0:(b + 1) * P - m0]
+                                  in_=w_bf[b][:].rearrange("p z m t -> p (z m t)"))
+            for z in range(PASSES):
+                w_codes[z, b] = codes[:, z * P:(z + 1) * P]
+                w_plane[z, b] = plane[:, z * P:(z + 1) * P]
 
-        gather_words(0, 0, 512, "picked0_0")
-        gather_words(0, 512, 512, "picked0_512")
-        quantize_w(0, 0, N, sb.tile([P, N], U32, name="codes0", align_bytes=64))
-        gather_words(1, 0, 512, "w_bf0_0")
-        quantize_w(1, 0, P, sb.tile([P, P], U32, name="codes1_0", align_bytes=64))
-        gather_words(1, 512, 256, "w_bf1_0")
-        gather_words(1, 768, 256, "picked1_768")
-        quantize_w(1, P, P, late.tile([P, P], U32, name="codes1_1", offset=0, align_bytes=64))
+        picked = [gather_words(0, WIDE, "picked0")]
+        quantize_w(0, sb.tile([P, PASSES * P], U32, name="w_codes0", align_bytes=64))
+        picked.append(gather_words(1, GROUPS, "w_bf0"))
+        quantize_w(1, late.tile([P, PASSES * P], U32, name="w_codes1", offset=0, align_bytes=64))
         rest = late.tile([P, V], F32, name="rest", offset=1024, align_bytes=64)
         nc.vector.tensor_scalar(rest[:], frac_t[:], -1.0, 1.0, MULT, ADD)
 
@@ -118,24 +120,20 @@ def tile_picked_lerp_gelu_p_kernel(tc, x_words, x_scales, w1, frac, offs, left, 
         def product(b, z, j0, n, bank=None):
             if z == 0:
                 acc[b, j0] = psum.tile([P, BANK], F32, name=f"acc{b}_{j0}", tag=bank)
-            first = j0 // 512 * 512 if z == 0 else j0
             nc.tensor.matmul_mx(out=acc[b, j0][:, 0:n],
                                 lhsT=w_codes[z, b].bitcast(FP8X4), lhsT_scale=w_plane[z, b],
-                                rhs=picked[z, first][:, j0 - first:j0 - first + n].bitcast(FP4X4),
-                                rhs_scale=x_plane[z][:, j0:j0 + n],
+                                rhs=picked[z][:, j0:j0 + n].bitcast(FP4X4), rhs_scale=x_plane[z][:, j0:j0 + n],
                                 start=(z == 0), stop=(z == PASSES - 1))
             if z == PASSES - 1:
                 nc.scalar.activation(y[b][:, j0:j0 + n], acc[b, j0][:, 0:n], GELU)
 
         for g, (j0, n) in enumerate(GROUPS):
             product(0, 0, j0, n, f"bank{g}")
-        product(1, 0, *GROUPS[0], "bank3")
         for j0, n in GROUPS:
             product(0, 1, j0, n)
-        for g in (1, 2):
-            product(1, 0, *GROUPS[g], f"bank{g - 1}")
-        for j0, n in GROUPS:
-            product(1, 1, j0, n)
+        for g, (j0, n) in enumerate(WIDE):
+            for z in range(PASSES):
+                product(1, z, j0, n, f"bank{g}")
 
         halves = [slice(0, HALF), slice(HALF, V)]
 

@@ -52,17 +52,17 @@ def tile_picked_lerp_gelu_p_kernel(tc, x_words, x_scales, w1, frac, offs, left, 
         nc.scalar.dma_start(out=scale_win[SCALE_ROW0:P, :].bitcast(I32),
                             in_=x_scales.rearrange("z q c -> (z q) c").bitcast(I32))
         nc.sync.dma_start(offs_t[:], offs)
-        nc.sync.dma_start(left_t[:], left)
-        nc.sync.dma_start(right_t[:], right)
         nc.vector.memset(scale_win[0:SCALE_ROW0, :].bitcast(I32), 0)
 
         word_win = [sb.tile([P, T], U16, name="word_win0", align_bytes=64),
                     late.tile([P, T], U16, name="word_win1", offset=0, align_bytes=64)]
         w_raw = [sb.tile([P, PACK, N], F32, name=f"w_raw{z}", align_bytes=64) for z in range(PASSES)]
         nc.sync.dma_start(out=word_win[0][:].bitcast(I32), in_=x_words[0].bitcast(I32))
+        nc.sync.dma_start(left_t[:], left)
+        nc.sync.dma_start(right_t[:], right)
         for z in range(PASSES):
-            nc.sync.dma_start(out=w_raw[z][:], in_=w1[z * K_PASS:(z + 1) * K_PASS, :].rearrange("(p t) m -> p t m", t=PACK))
-        nc.sync.dma_start(out=word_win[1][:].bitcast(I32), in_=x_words[1].bitcast(I32))
+            nc.scalar.dma_start(out=w_raw[z][:], in_=w1[z * K_PASS:(z + 1) * K_PASS, :].rearrange("(p t) m -> p t m", t=PACK))
+        nc.scalar.dma_start(out=word_win[1][:].bitcast(I32), in_=x_words[1].bitcast(I32))
 
         warm = sb.tile([P, 8], F32, name="warm")
         warm_out = sb.tile([P, 8], F32, name="warm_out")
@@ -78,8 +78,9 @@ def tile_picked_lerp_gelu_p_kernel(tc, x_words, x_scales, w1, frac, offs, left, 
         for z in range(PASSES):
             row0 = SCALE_ROW0 + PASS_ROWS * z
             for r in range(QUADRANT_ROWS):
-                nc.sync.dma_start(out=x_plane[z][r:P:QUADRANT, :].bitcast(I32),
-                                  in_=picked_scales[row0 + r:row0 + PASS_ROWS:QUADRANT_ROWS, :].bitcast(I32))
+                queue = nc.gpsimd if (z, r) == (PASSES - 1, QUADRANT_ROWS - 1) else nc.sync
+                queue.dma_start(out=x_plane[z][r:P:QUADRANT, :].bitcast(I32),
+                                in_=picked_scales[row0 + r:row0 + PASS_ROWS:QUADRANT_ROWS, :].bitcast(I32))
 
         frac_t = sb.tile([P, V], F32, name="frac_t", tag="scales_then_frac", align_bytes=64)
         nc.sync.dma_start(out=frac_t[:], in_=frac)

@@ -64,11 +64,6 @@ def tile_picked_lerp_gelu_p_kernel(tc, x_words, x_scales, w1, frac, offs, left, 
             nc.scalar.dma_start(out=w_raw[z][:], in_=w1[z * K_PASS:(z + 1) * K_PASS, :].rearrange("(p t) m -> p t m", t=PACK))
         nc.scalar.dma_start(out=word_win[1][:].bitcast(I32), in_=x_words[1].bitcast(I32))
 
-        warm = sb.tile([P, 8], F32, name="warm")
-        warm_out = sb.tile([P, 8], F32, name="warm_out")
-        nc.vector.memset(warm[:], 0.0)
-        nc.scalar.activation(warm_out[:], warm[:], GELU)
-
         x_plane = [sb.tile([P, S], U8, name=f"x_plane{z}", align_bytes=64) for z in range(PASSES)]
         for z in range(PASSES):
             nc.vector.memset(x_plane[z][:].bitcast(I32), 0)

@@ -16,11 +16,14 @@ SCALE_ROW0 = P - PASSES * PASS_ROWS
 RUN = 4
 BANK = 512
 HALF = V // 2
-OWN = 128
+OWN = 0
+SHARE = 384
 FLOPS = 2 * K * N * S
 
-GROUPS = ((0, 512), (512, 256), (768, 256))
-WIDE = ((0, 512), (512, 512))
+GROUPS = ((0, 512), (512, 256), (768, 128), (896, 128))
+WIDE = ((0, 256), (256, 256), (512, 256), (768, 256))
+CUTS0 = ((0, 512), (512, 512))
+CUTS1 = ((0, 512), (512, 256), (768, 256))
 
 F32 = mybir.dt.float32
 BF16 = mybir.dt.bfloat16
@@ -95,18 +98,19 @@ def tile_picked_lerp_gelu_p_kernel(tc, x_words, x_scales, w1, frac, offs, left, 
                                       word_win[z][:].indirect(offs_t[:, j0 // STRIPE:(j0 + n) // STRIPE]))
             return tile
 
-        def quantize_w(b, codes):
+        def quantize_w(b, step, codes):
             plane = sb.tile([P, PASSES * P], U8, name=f"w_plane{b}", align_bytes=64)
-            nc.vector.quantize_mx(out=codes[:].bitcast(FP8X4), scales=plane[:],
-                                  in_=w_bf[b][:].rearrange("p z m t -> p (z m t)"))
+            for z0 in range(0, PASSES, step):
+                nc.vector.quantize_mx(out=codes[:, z0 * P:(z0 + step) * P].bitcast(FP8X4), scales=plane[:, z0 * P:(z0 + step) * P],
+                                      in_=w_bf[b][:, z0:z0 + step].rearrange("p z m t -> p (z m t)"))
             for z in range(PASSES):
                 w_codes[z, b] = codes[:, z * P:(z + 1) * P]
                 w_plane[z, b] = plane[:, z * P:(z + 1) * P]
 
-        picked = [gather_words(0, WIDE, "picked0")]
-        quantize_w(0, sb.tile([P, PASSES * P], U32, name="w_codes0", align_bytes=64))
-        picked.append(gather_words(1, GROUPS, "w_bf0"))
-        quantize_w(1, late.tile([P, PASSES * P], U32, name="w_codes1", offset=0, align_bytes=64))
+        picked = [gather_words(0, CUTS0, "picked0")]
+        quantize_w(0, PASSES, sb.tile([P, PASSES * P], U32, name="w_codes0", align_bytes=64))
+        picked.append(gather_words(1, CUTS1, "w_bf0"))
+        quantize_w(1, 1, late.tile([P, PASSES * P], U32, name="w_codes1", offset=0, align_bytes=64))
         rest = late.tile([P, V], F32, name="rest", offset=1024, align_bytes=64)
         nc.vector.tensor_scalar(rest[:], frac_t[:], -1.0, 1.0, MULT, ADD)
 
@@ -140,10 +144,12 @@ def tile_picked_lerp_gelu_p_kernel(tc, x_words, x_scales, w1, frac, offs, left, 
         hi_w = [sb.tile([P, V], F32, name=f"hi_w{b}", align_bytes=64) for b in range(ROW_BLOCKS)]
         res = [sb.tile([P, V], F32, name=f"res{b}", align_bytes=64) for b in range(ROW_BLOCKS)]
         lo = sb.tile([P, V], F32, name="lo", align_bytes=64)
-        hi = sb.tile([P, HALF], F32, name="hi", align_bytes=64)
+        hi = sb.tile([P, SHARE], F32, name="hi", align_bytes=64)
+        pieces = [slice(HALF, SHARE), slice(0, HALF)]
 
         nc.scalar.activation(lo[:], y[1][:].indirect(left_t[:]), COPY)
-        nc.scalar.activation(hi[:], y[1][:].indirect(entries(right_t, halves[0])), COPY)
+        for cols in pieces:
+            nc.scalar.activation(hi[:, cols], y[1][:].indirect(entries(right_t, cols)), COPY)
 
         nc.vector.tensor_tensor(lo_w[0][:], y[0][:].indirect(left_t[:]), rest[:], MULT)
         for cols in halves:
@@ -151,9 +157,10 @@ def tile_picked_lerp_gelu_p_kernel(tc, x_words, x_scales, w1, frac, offs, left, 
         for cols in halves:
             nc.vector.tensor_tensor(res[0][:, cols], lo_w[0][:, cols], hi_w[0][:, cols], ADD)
         nc.sync.dma_start(out=out[0:P, :], in_=res[0][:])
-        nc.vector.tensor_tensor(hi_w[1][:, halves[1]], y[1][:].indirect(entries(right_t, halves[1])), frac_t[:, halves[1]], MULT)
+        nc.vector.tensor_tensor(hi_w[1][:, SHARE:V], y[1][:].indirect(entries(right_t, slice(SHARE, V))), frac_t[:, SHARE:V], MULT)
         nc.vector.tensor_tensor(lo_w[1][:], lo[:], rest[:], MULT)
-        nc.vector.tensor_tensor(hi_w[1][:, halves[0]], hi[:], frac_t[:, halves[0]], MULT)
+        for cols in pieces:
+            nc.vector.tensor_tensor(hi_w[1][:, cols], hi[:, cols], frac_t[:, cols], MULT)
         for cols in reversed(halves):
             nc.vector.tensor_tensor(res[1][:, cols], lo_w[1][:, cols], hi_w[1][:, cols], ADD)
             nc.sync.dma_start(out=out[P:2 * P, cols], in_=res[1][:, cols])

@@ -20,10 +20,8 @@ OWN = 0
 SHARE = 384
 FLOPS = 2 * K * N * S
 
-GROUPS = ((0, 512), (512, 256), (768, 128), (896, 128))
+GROUPS = ((0, 256), (256, 256), (512, 256), (768, 128), (896, 128))
 WIDE = ((0, 256), (256, 256), (512, 256), (768, 256))
-CUTS0 = ((0, 512), (512, 512))
-CUTS1 = ((0, 512), (512, 256), (768, 256))
 
 F32 = mybir.dt.float32
 BF16 = mybir.dt.bfloat16
@@ -44,7 +42,6 @@ def tile_picked_lerp_gelu_p_kernel(tc, x_words, x_scales, w1, frac, offs, left, 
     with ExitStack() as ctx:
         lists = ctx.enter_context(tc.tile_pool(name="lists", bufs=1))
         sb = ctx.enter_context(tc.tile_pool(name="sb", bufs=1))
-        late = ctx.enter_context(tc.tile_pool(name="late", bufs=1))
         psum = ctx.enter_context(tc.psum_pool(name="psum", bufs=1))
 
         offs_t = lists.tile([P, S // STRIPE], U16, name="offs_t")
@@ -58,8 +55,8 @@ def tile_picked_lerp_gelu_p_kernel(tc, x_words, x_scales, w1, frac, offs, left, 
         nc.vector.memset(scale_win[0:SCALE_ROW0, :].bitcast(I32), 0)
 
         word_win = [sb.tile([P, T], U16, name="word_win0", align_bytes=64),
-                    late.tile([P, T], U16, name="word_win1", offset=0, align_bytes=64)]
-        w_raw = [sb.tile([P, PACK, N], F32, name=f"w_raw{z}", align_bytes=64) for z in range(PASSES)]
+                    sb.tile([P, T], U16, name="word_win1", align_bytes=64)]
+        w_raw = [sb.tile([P, PACK, N], F32, name=f"w_raw{z}", tag=f"w_raw{z}", align_bytes=64) for z in range(PASSES)]
         nc.sync.dma_start(out=word_win[0][:].bitcast(I32), in_=x_words[0].bitcast(I32))
         nc.sync.dma_start(left_t[:], left)
         nc.sync.dma_start(right_t[:], right)
@@ -91,27 +88,33 @@ def tile_picked_lerp_gelu_p_kernel(tc, x_words, x_scales, w1, frac, offs, left, 
 
         w_codes, w_plane = {}, {}
 
-        def gather_words(z, cuts, tag):
-            tile = sb.tile([P, S], U16, name=f"picked{z}", tag=tag, align_bytes=64)
-            for j0, n in cuts:
-                nc.vector.tensor_copy(tile[:, j0:j0 + n],
-                                      word_win[z][:].indirect(offs_t[:, j0 // STRIPE:(j0 + n) // STRIPE]))
-            return tile
+        picked = {}
 
-        def quantize_w(b, step, codes):
-            plane = sb.tile([P, PASSES * P], U8, name=f"w_plane{b}", align_bytes=64)
-            for z0 in range(0, PASSES, step):
-                nc.vector.quantize_mx(out=codes[:, z0 * P:(z0 + step) * P].bitcast(FP8X4), scales=plane[:, z0 * P:(z0 + step) * P],
-                                      in_=w_bf[b][:, z0:z0 + step].rearrange("p z m t -> p (z m t)"))
-            for z in range(PASSES):
-                w_codes[z, b] = codes[:, z * P:(z + 1) * P]
-                w_plane[z, b] = plane[:, z * P:(z + 1) * P]
+        def gather_words(z, j0, cut, tag):
+            tile = sb.tile([P, BANK], U16, name=f"picked{z}_{j0}", tag=tag, align_bytes=64)
+            for j in range(0, BANK, cut):
+                nc.vector.tensor_copy(tile[:, j:j + cut],
+                                      word_win[z][:].indirect(offs_t[:, (j0 + j) // STRIPE:(j0 + j + cut) // STRIPE]))
+            picked[z, j0 // BANK] = tile
 
-        picked = [gather_words(0, CUTS0, "picked0")]
-        quantize_w(0, PASSES, sb.tile([P, PASSES * P], U32, name="w_codes0", align_bytes=64))
-        picked.append(gather_words(1, CUTS1, "w_bf0"))
-        quantize_w(1, 1, late.tile([P, PASSES * P], U32, name="w_codes1", offset=0, align_bytes=64))
-        rest = late.tile([P, V], F32, name="rest", offset=1024, align_bytes=64)
+        codes = [sb.tile([P, PASSES * P], U32, name=f"w_codes{b}", align_bytes=64) for b in range(ROW_BLOCKS)]
+        plane = [sb.tile([P, PASSES * P], U8, name=f"w_plane{b}", align_bytes=64) for b in range(ROW_BLOCKS)]
+
+        def quantize_w(b, z0, z1):
+            nc.vector.quantize_mx(out=codes[b][:, z0 * P:z1 * P].bitcast(FP8X4), scales=plane[b][:, z0 * P:z1 * P],
+                                  in_=w_bf[b][:, z0:z1].rearrange("p z m t -> p (z m t)"))
+            for z in range(z0, z1):
+                w_codes[z, b] = codes[b][:, z * P:(z + 1) * P]
+                w_plane[z, b] = plane[b][:, z * P:(z + 1) * P]
+
+        gather_words(0, 0, BANK, "picked00")
+        gather_words(0, BANK, BANK, "picked01")
+        quantize_w(0, 0, 1)
+        gather_words(1, 0, BANK, "w_raw0")
+        quantize_w(0, 1, 2)
+        gather_words(1, BANK, BANK // 2, "w_raw1")
+        quantize_w(1, 0, 2)
+        rest = sb.tile([P, V], F32, name="rest", align_bytes=64)
         nc.vector.tensor_scalar(rest[:], frac_t[:], -1.0, 1.0, MULT, ADD)
 
         y = [sb.tile([P, S], F32, name=f"y{b}", align_bytes=64) for b in range(ROW_BLOCKS)]
@@ -122,7 +125,7 @@ def tile_picked_lerp_gelu_p_kernel(tc, x_words, x_scales, w1, frac, offs, left, 
                 acc[b, j0] = psum.tile([P, BANK], F32, name=f"acc{b}_{j0}", tag=bank)
             nc.tensor.matmul_mx(out=acc[b, j0][:, 0:n],
                                 lhsT=w_codes[z, b].bitcast(FP8X4), lhsT_scale=w_plane[z, b],
-                                rhs=picked[z][:, j0:j0 + n].bitcast(FP4X4), rhs_scale=x_plane[z][:, j0:j0 + n],
+                                rhs=picked[z, j0 // BANK][:, j0 % BANK:j0 % BANK + n].bitcast(FP4X4), rhs_scale=x_plane[z][:, j0:j0 + n],
                                 start=(z == 0), stop=(z == PASSES - 1))
             if z == PASSES - 1:
                 nc.scalar.activation(y[b][:, j0:j0 + n], acc[b, j0][:, 0:n], GELU)
@@ -145,22 +148,19 @@ def tile_picked_lerp_gelu_p_kernel(tc, x_words, x_scales, w1, frac, offs, left, 
         res = [sb.tile([P, V], F32, name=f"res{b}", align_bytes=64) for b in range(ROW_BLOCKS)]
         lo = sb.tile([P, V], F32, name="lo", align_bytes=64)
         hi = sb.tile([P, SHARE], F32, name="hi", align_bytes=64)
-        pieces = [slice(HALF, SHARE), slice(0, HALF)]
 
-        nc.scalar.activation(lo[:], y[1][:].indirect(left_t[:]), COPY)
-        for cols in pieces:
-            nc.scalar.activation(hi[:, cols], y[1][:].indirect(entries(right_t, cols)), COPY)
+        nc.scalar.activation(hi[:], y[1][:].indirect(entries(right_t, slice(0, SHARE))), COPY)
+        for cols in reversed(halves):
+            nc.scalar.activation(lo[:, cols], y[1][:].indirect(entries(left_t, cols)), COPY)
 
         nc.vector.tensor_tensor(lo_w[0][:], y[0][:].indirect(left_t[:]), rest[:], MULT)
-        for cols in halves:
-            nc.vector.tensor_tensor(hi_w[0][:, cols], y[0][:].indirect(entries(right_t, cols)), frac_t[:, cols], MULT)
-        for cols in halves:
-            nc.vector.tensor_tensor(res[0][:, cols], lo_w[0][:, cols], hi_w[0][:, cols], ADD)
-        nc.sync.dma_start(out=out[0:P, :], in_=res[0][:])
+        nc.vector.tensor_tensor(hi_w[0][:], y[0][:].indirect(right_t[:]), frac_t[:], MULT)
         nc.vector.tensor_tensor(hi_w[1][:, SHARE:V], y[1][:].indirect(entries(right_t, slice(SHARE, V))), frac_t[:, SHARE:V], MULT)
-        nc.vector.tensor_tensor(lo_w[1][:], lo[:], rest[:], MULT)
-        for cols in pieces:
-            nc.vector.tensor_tensor(hi_w[1][:, cols], hi[:, cols], frac_t[:, cols], MULT)
+        nc.vector.tensor_tensor(res[0][:], lo_w[0][:], hi_w[0][:], ADD)
+        nc.sync.dma_start(out=out[0:P, :], in_=res[0][:])
+        nc.vector.tensor_tensor(hi_w[1][:, 0:SHARE], hi[:], frac_t[:, 0:SHARE], MULT)
+        for cols in reversed(halves):
+            nc.vector.tensor_tensor(lo_w[1][:, cols], lo[:, cols], rest[:, cols], MULT)
         for cols in reversed(halves):
             nc.vector.tensor_tensor(res[1][:, cols], lo_w[1][:, cols], hi_w[1][:, cols], ADD)
             nc.sync.dma_start(out=out[P:2 * P, cols], in_=res[1][:, cols])

@@ -73,9 +73,8 @@ def tile_picked_lerp_gelu_p_kernel(tc, x_words, x_scales, w1, frac, offs, left, 
         for z in range(PASSES):
             row0 = SCALE_ROW0 + PASS_ROWS * z
             for r in range(QUADRANT_ROWS):
-                queue = nc.gpsimd if (z, r) == (PASSES - 1, QUADRANT_ROWS - 1) else nc.sync
-                queue.dma_start(out=x_plane[z][r:P:QUADRANT, :].bitcast(I32),
-                                in_=picked_scales[row0 + r:row0 + PASS_ROWS:QUADRANT_ROWS, :].bitcast(I32))
+                nc.sync.dma_start(out=x_plane[z][r:P:QUADRANT, :].bitcast(I32),
+                                  in_=picked_scales[row0 + r:row0 + PASS_ROWS:QUADRANT_ROWS, :].bitcast(I32))
 
         frac_t = sb.tile([P, V], F32, name="frac_t", tag="scales_then_frac", align_bytes=64)
         nc.sync.dma_start(out=frac_t[:], in_=frac)
@@ -153,8 +152,8 @@ def tile_picked_lerp_gelu_p_kernel(tc, x_words, x_scales, w1, frac, offs, left, 
         for cols in reversed(halves):
             nc.scalar.activation(lo[:, cols], y[1][:].indirect(entries(left_t, cols)), COPY)
 
-        nc.vector.tensor_tensor(lo_w[0][:], y[0][:].indirect(left_t[:]), rest[:], MULT)
         nc.vector.tensor_tensor(hi_w[0][:], y[0][:].indirect(right_t[:]), frac_t[:], MULT)
+        nc.vector.tensor_tensor(lo_w[0][:], y[0][:].indirect(left_t[:]), rest[:], MULT)
         nc.vector.tensor_tensor(hi_w[1][:, SHARE:V], y[1][:].indirect(entries(right_t, slice(SHARE, V))), frac_t[:, SHARE:V], MULT)
         nc.vector.tensor_tensor(res[0][:], lo_w[0][:], hi_w[0][:], ADD)
         nc.sync.dma_start(out=out[0:P, :], in_=res[0][:])

@@ -80,8 +80,8 @@ def tile_picked_lerp_gelu_p_kernel(tc, x_words, x_scales, w1, frac, offs, left, 
         nc.sync.dma_start(out=frac_t[:], in_=frac)
 
         w_bf = [sb.tile([P, PASSES, P, PACK], BF16, name=f"w_bf{b}", tag=f"w_bf{b}", align_bytes=64) for b in range(ROW_BLOCKS)]
-        for b in range(ROW_BLOCKS):
-            for z in range(PASSES):
+        for z in range(PASSES):
+            for b in range(ROW_BLOCKS):
                 nc.scalar.copy(w_bf[b][:, z].rearrange("p (c i) t -> p c t i", i=RUN),
                                w_raw[z][:, :, b * P:(b + 1) * P].rearrange("p t (c i) -> p c t i", i=RUN))
 

@@ -160,6 +160,6 @@ def tile_picked_lerp_gelu_p_kernel(tc, x_words, x_scales, w1, frac, offs, left, 
         nc.vector.tensor_tensor(hi_w[1][:, 0:SHARE], hi[:], frac_t[:, 0:SHARE], MULT)
         for cols in reversed(halves):
             nc.vector.tensor_tensor(lo_w[1][:, cols], lo[:, cols], rest[:, cols], MULT)
-        for cols in reversed(halves):
+        for cols in (halves[1], slice(HALF // 2, HALF), slice(0, HALF // 2)):
             nc.vector.tensor_tensor(res[1][:, cols], lo_w[1][:, cols], hi_w[1][:, cols], ADD)
             nc.sync.dma_start(out=out[P:2 * P, cols], in_=res[1][:, cols])

@@ -50,7 +50,7 @@ def tile_picked_lerp_gelu_p_kernel(tc, x_words, x_scales, w1, frac, offs, left, 
 
         scale_win = sb.tile([P, T], U8, name="scale_win", tag="scales_then_frac", align_bytes=64)
         nc.scalar.dma_start(out=scale_win[SCALE_ROW0:P, :].bitcast(I32),
-                            in_=x_scales.rearrange("z q c -> (z q) c").bitcast(I32))
+                            in_=x_scales.rearrange("z q c -> q z c").bitcast(I32))
         nc.sync.dma_start(offs_t[:], offs)
         nc.vector.memset(scale_win[0:SCALE_ROW0, :].bitcast(I32), 0)
 
@@ -64,17 +64,16 @@ def tile_picked_lerp_gelu_p_kernel(tc, x_words, x_scales, w1, frac, offs, left, 
             nc.scalar.dma_start(out=w_raw[z][:], in_=w1[z * K_PASS:(z + 1) * K_PASS, :].rearrange("(p t) m -> p t m", t=PACK))
         nc.scalar.dma_start(out=word_win[1][:].bitcast(I32), in_=x_words[1].bitcast(I32))
 
-        x_plane = [sb.tile([P, S], U8, name=f"x_plane{z}", align_bytes=64) for z in range(PASSES)]
-        for z in range(PASSES):
-            nc.vector.memset(x_plane[z][:].bitcast(I32), 0)
+        x_plane = sb.tile([P, PASSES, S], U8, name="x_plane", align_bytes=64)
+        nc.vector.memset(x_plane[:].bitcast(I32), 0)
 
         picked_scales = sb.tile([P, S], U8, name="picked_scales", align_bytes=64)
         nc.vector.tensor_copy(picked_scales[:], scale_win[:].indirect(offs_t[:]))
-        for z in range(PASSES):
-            row0 = SCALE_ROW0 + PASS_ROWS * z
-            for r in range(QUADRANT_ROWS):
-                nc.sync.dma_start(out=x_plane[z][r:P:QUADRANT, :].bitcast(I32),
-                                  in_=picked_scales[row0 + r:row0 + PASS_ROWS:QUADRANT_ROWS, :].bitcast(I32))
+        rows = PASSES * QUADRANT_ROWS
+        for q in range(P // QUADRANT):
+            row0 = SCALE_ROW0 + rows * q
+            nc.sync.dma_start(out=x_plane[QUADRANT * q:QUADRANT * q + QUADRANT_ROWS].bitcast(I32),
+                              in_=picked_scales[row0:row0 + rows, :].bitcast(I32))
 
         frac_t = sb.tile([P, V], F32, name="frac_t", tag="scales_then_frac", align_bytes=64)
         nc.sync.dma_start(out=frac_t[:], in_=frac)
@@ -124,7 +123,7 @@ def tile_picked_lerp_gelu_p_kernel(tc, x_words, x_scales, w1, frac, offs, left, 
                 acc[b, j0] = psum.tile([P, BANK], F32, name=f"acc{b}_{j0}", tag=bank)
             nc.tensor.matmul_mx(out=acc[b, j0][:, 0:n],
                                 lhsT=w_codes[z, b].bitcast(FP8X4), lhsT_scale=w_plane[z, b],
-                                rhs=picked[z, j0 // BANK][:, j0 % BANK:j0 % BANK + n].bitcast(FP4X4), rhs_scale=x_plane[z][:, j0:j0 + n],
+                                rhs=picked[z, j0 // BANK][:, j0 % BANK:j0 % BANK + n].bitcast(FP4X4), rhs_scale=x_plane[:, z, j0:j0 + n],
                                 start=(z == 0), stop=(z == PASSES - 1))
             if z == PASSES - 1:
                 nc.scalar.activation(y[b][:, j0:j0 + n], acc[b, j0][:, 0:n], GELU)
@@ -160,6 +159,6 @@ def tile_picked_lerp_gelu_p_kernel(tc, x_words, x_scales, w1, frac, offs, left, 
         nc.vector.tensor_tensor(hi_w[1][:, 0:SHARE], hi[:], frac_t[:, 0:SHARE], MULT)
         for cols in reversed(halves):
             nc.vector.tensor_tensor(lo_w[1][:, cols], lo[:, cols], rest[:, cols], MULT)
-        for cols in (halves[1], slice(HALF // 2, HALF), slice(0, HALF // 2)):
+        for cols in reversed(halves):
             nc.vector.tensor_tensor(res[1][:, cols], lo_w[1][:, cols], hi_w[1][:, cols], ADD)
             nc.sync.dma_start(out=out[P:2 * P, cols], in_=res[1][:, cols])

@@ -16,8 +16,8 @@ SCALE_ROW0 = P - PASSES * PASS_ROWS
 RUN = 4
 BANK = 512
 HALF = V // 2
-OWN = 0
-SHARE = 384
+LENT = 128
+OWN = 192
 FLOPS = 2 * K * N * S
 
 GROUPS = ((0, 256), (256, 256), (512, 256), (768, 128), (896, 128))
@@ -75,8 +75,8 @@ def tile_picked_lerp_gelu_p_kernel(tc, x_words, x_scales, w1, frac, offs, left, 
             nc.sync.dma_start(out=x_plane[QUADRANT * q:QUADRANT * q + QUADRANT_ROWS].bitcast(I32),
                               in_=picked_scales[row0:row0 + rows, :].bitcast(I32))
 
-        frac_t = sb.tile([P, V], F32, name="frac_t", tag="scales_then_frac", align_bytes=64)
-        nc.sync.dma_start(out=frac_t[:], in_=frac)
+        factor = sb.tile([P, 2 * V], F32, name="factor", tag="scales_then_frac", align_bytes=64)
+        nc.sync.dma_start(out=factor[:, 0:V], in_=frac)
 
         w_bf = [sb.tile([P, PASSES, P, PACK], BF16, name=f"w_bf{b}", tag=f"w_bf{b}", align_bytes=64) for b in range(ROW_BLOCKS)]
         for z in range(PASSES):
@@ -112,8 +112,7 @@ def tile_picked_lerp_gelu_p_kernel(tc, x_words, x_scales, w1, frac, offs, left, 
         quantize_w(0, 1, 2)
         gather_words(1, BANK, BANK // 2, "w_raw1")
         quantize_w(1, 0, 2)
-        rest = sb.tile([P, V], F32, name="rest", align_bytes=64)
-        nc.vector.tensor_scalar(rest[:], frac_t[:], -1.0, 1.0, MULT, ADD)
+        nc.vector.tensor_scalar(factor[:, V:2 * V], factor[:, 0:V], -1.0, 1.0, MULT, ADD)
 
         y = [sb.tile([P, S], F32, name=f"y{b}", align_bytes=64) for b in range(ROW_BLOCKS)]
         acc = {}
@@ -136,29 +135,28 @@ def tile_picked_lerp_gelu_p_kernel(tc, x_words, x_scales, w1, frac, offs, left, 
             for z in range(PASSES):
                 product(1, z, j0, n, f"bank{g}")
 
-        halves = [slice(0, HALF), slice(HALF, V)]
+        def fetched(b, lst, c0, c1):
+            return y[b][:].indirect(lst[:, c0 // STRIPE:c1 // STRIPE])
 
-        def entries(lst, cols):
-            return lst[:, cols.start // STRIPE:cols.stop // STRIPE]
-
-        lo_w = [sb.tile([P, V], F32, name=f"lo_w{b}", align_bytes=64) for b in range(ROW_BLOCKS)]
-        hi_w = [sb.tile([P, V], F32, name=f"hi_w{b}", align_bytes=64) for b in range(ROW_BLOCKS)]
+        term = [sb.tile([P, 2 * V], F32, name=f"term{b}", align_bytes=64) for b in range(ROW_BLOCKS)]
         res = [sb.tile([P, V], F32, name=f"res{b}", align_bytes=64) for b in range(ROW_BLOCKS)]
-        lo = sb.tile([P, V], F32, name="lo", align_bytes=64)
-        hi = sb.tile([P, SHARE], F32, name="hi", align_bytes=64)
+        plain = sb.tile([P, 2 * V], F32, name="plain", align_bytes=64)
+        lent = sb.tile([P, LENT], F32, name="lent", tag="picked01", align_bytes=64)
 
-        nc.scalar.activation(hi[:], y[1][:].indirect(entries(right_t, slice(0, SHARE))), COPY)
-        for cols in reversed(halves):
-            nc.scalar.activation(lo[:, cols], y[1][:].indirect(entries(left_t, cols)), COPY)
+        nc.scalar.activation(lent[:], fetched(0, left_t, 0, LENT), COPY)
+        nc.scalar.activation(plain[:, OWN:V], fetched(1, right_t, OWN, V), COPY)
+        nc.scalar.activation(plain[:, V:V + HALF], fetched(1, left_t, 0, HALF), COPY)
+        nc.scalar.activation(plain[:, V + HALF:2 * V], fetched(1, left_t, HALF, V), COPY)
 
-        nc.vector.tensor_tensor(hi_w[0][:], y[0][:].indirect(right_t[:]), frac_t[:], MULT)
-        nc.vector.tensor_tensor(lo_w[0][:], y[0][:].indirect(left_t[:]), rest[:], MULT)
-        nc.vector.tensor_tensor(hi_w[1][:, SHARE:V], y[1][:].indirect(entries(right_t, slice(SHARE, V))), frac_t[:, SHARE:V], MULT)
-        nc.vector.tensor_tensor(res[0][:], lo_w[0][:], hi_w[0][:], ADD)
+        nc.vector.tensor_tensor(term[0][:, 0:V], fetched(0, right_t, 0, V), factor[:, 0:V], MULT)
+        nc.vector.tensor_tensor(term[0][:, V + LENT:2 * V], fetched(0, left_t, LENT, V), factor[:, V + LENT:2 * V], MULT)
+        nc.vector.tensor_tensor(term[0][:, V:V + LENT], lent[:], factor[:, V:V + LENT], MULT)
+        nc.vector.tensor_tensor(term[1][:, 0:OWN], fetched(1, right_t, 0, OWN), factor[:, 0:OWN], MULT)
+        for c0, c1 in ((LENT, V), (0, LENT)):
+            nc.vector.tensor_tensor(res[0][:, c0:c1], term[0][:, c0:c1], term[0][:, V + c0:V + c1], ADD)
         nc.sync.dma_start(out=out[0:P, :], in_=res[0][:])
-        nc.vector.tensor_tensor(hi_w[1][:, 0:SHARE], hi[:], frac_t[:, 0:SHARE], MULT)
-        for cols in reversed(halves):
-            nc.vector.tensor_tensor(lo_w[1][:, cols], lo[:, cols], rest[:, cols], MULT)
-        for cols in reversed(halves):
-            nc.vector.tensor_tensor(res[1][:, cols], lo_w[1][:, cols], hi_w[1][:, cols], ADD)
-            nc.sync.dma_start(out=out[P:2 * P, cols], in_=res[1][:, cols])
+        nc.vector.tensor_tensor(term[1][:, OWN:V + HALF], plain[:, OWN:V + HALF], factor[:, OWN:V + HALF], MULT)
+        nc.vector.tensor_tensor(term[1][:, V + HALF:2 * V], plain[:, V + HALF:2 * V], factor[:, V + HALF:2 * V], MULT)
+        for c0 in (0, HALF):
+            nc.vector.tensor_tensor(res[1][:, c0:c0 + HALF], term[1][:, c0:c0 + HALF], term[1][:, V + c0:V + c0 + HALF], ADD)
+            nc.sync.dma_start(out=out[P:2 * P, c0:c0 + HALF], in_=res[1][:, c0:c0 + HALF])

from contextlib import ExitStack

import concourse.mybir as mybir

K, T, S, V, N = 1024, 2048, 1024, 512, 256
P = 128
PACK = 4
K_PASS = P * PACK
PASSES = K // K_PASS
ROW_BLOCKS = N // P
STRIPE = 16
QUADRANT = 32
QUADRANT_ROWS = 4
PASS_ROWS = K_PASS // 32
SCALE_ROW0 = P - PASSES * PASS_ROWS
RUN = 4
BANK = 512
HALF = V // 2
LENT = 128
OWN = 192
FLOPS = 2 * K * N * S

GROUPS = ((0, 256), (256, 256), (512, 256), (768, 128), (896, 128))
WIDE = ((0, 256), (256, 256), (512, 256), (768, 256))

F32 = mybir.dt.float32
BF16 = mybir.dt.bfloat16
I32 = mybir.dt.int32
U32 = mybir.dt.uint32
U16 = mybir.dt.uint16
U8 = mybir.dt.uint8
FP8X4 = mybir.dt.float8_e4m3fn_x4
FP4X4 = mybir.dt.float4_e2m1fn_x4
GELU = mybir.ActivationFunctionType.Gelu_apprx_tanh
COPY = mybir.ActivationFunctionType.Copy
MULT = mybir.AluOpType.mult
ADD = mybir.AluOpType.add


def tile_picked_lerp_gelu_p_kernel(tc, x_words, x_scales, w1, frac, offs, left, right, out):
    nc = tc.nc
    with ExitStack() as ctx:
        lists = ctx.enter_context(tc.tile_pool(name="lists", bufs=1))
        sb = ctx.enter_context(tc.tile_pool(name="sb", bufs=1))
        psum = ctx.enter_context(tc.psum_pool(name="psum", bufs=1))

        offs_t = lists.tile([P, S // STRIPE], U16, name="offs_t")
        left_t = lists.tile([P, V // STRIPE], U16, name="left_t")
        right_t = lists.tile([P, V // STRIPE], U16, name="right_t")

        scale_win = sb.tile([P, T], U8, name="scale_win", tag="scales_then_frac", align_bytes=64)
        nc.scalar.dma_start(out=scale_win[SCALE_ROW0:P, :].bitcast(I32),
                            in_=x_scales.rearrange("z q c -> q z c").bitcast(I32))
        nc.sync.dma_start(offs_t[:], offs)
        nc.vector.memset(scale_win[0:SCALE_ROW0, :].bitcast(I32), 0)

        word_win = [sb.tile([P, T], U16, name="word_win0", align_bytes=64),
                    sb.tile([P, T], U16, name="word_win1", align_bytes=64)]
        w_raw = [sb.tile([P, PACK, N], F32, name=f"w_raw{z}", tag=f"w_raw{z}", align_bytes=64) for z in range(PASSES)]
        nc.sync.dma_start(out=word_win[0][:].bitcast(I32), in_=x_words[0].bitcast(I32))
        nc.sync.dma_start(left_t[:], left)
        nc.sync.dma_start(right_t[:], right)
        for z in range(PASSES):
            nc.scalar.dma_start(out=w_raw[z][:], in_=w1[z * K_PASS:(z + 1) * K_PASS, :].rearrange("(p t) m -> p t m", t=PACK))
        nc.scalar.dma_start(out=word_win[1][:].bitcast(I32), in_=x_words[1].bitcast(I32))

        x_plane = sb.tile([P, PASSES, S], U8, name="x_plane", align_bytes=64)
        nc.vector.memset(x_plane[:].bitcast(I32), 0)

        picked_scales = sb.tile([P, S], U8, name="picked_scales", align_bytes=64)
        nc.vector.tensor_copy(picked_scales[:], scale_win[:].indirect(offs_t[:]))
        rows = PASSES * QUADRANT_ROWS
        for q in range(P // QUADRANT):
            row0 = SCALE_ROW0 + rows * q
            nc.sync.dma_start(out=x_plane[QUADRANT * q:QUADRANT * q + QUADRANT_ROWS].bitcast(I32),
                              in_=picked_scales[row0:row0 + rows, :].bitcast(I32))

        factor = sb.tile([P, 2 * V], F32, name="factor", tag="scales_then_frac", align_bytes=64)
        nc.sync.dma_start(out=factor[:, 0:V], in_=frac)

        w_bf = [sb.tile([P, PASSES, P, PACK], BF16, name=f"w_bf{b}", tag=f"w_bf{b}", align_bytes=64) for b in range(ROW_BLOCKS)]
        for z in range(PASSES):
            for b in range(ROW_BLOCKS):
                nc.scalar.copy(w_bf[b][:, z].rearrange("p (c i) t -> p c t i", i=RUN),
                               w_raw[z][:, :, b * P:(b + 1) * P].rearrange("p t (c i) -> p c t i", i=RUN))

        w_codes, w_plane = {}, {}

        picked = {}

        def gather_words(z, j0, cut, tag):
            tile = sb.tile([P, BANK], U16, name=f"picked{z}_{j0}", tag=tag, align_bytes=64)
            for j in range(0, BANK, cut):
                nc.vector.tensor_copy(tile[:, j:j + cut],
                                      word_win[z][:].indirect(offs_t[:, (j0 + j) // STRIPE:(j0 + j + cut) // STRIPE]))
            picked[z, j0 // BANK] = tile

        codes = [sb.tile([P, PASSES * P], U32, name=f"w_codes{b}", align_bytes=64) for b in range(ROW_BLOCKS)]
        plane = [sb.tile([P, PASSES * P], U8, name=f"w_plane{b}", align_bytes=64) for b in range(ROW_BLOCKS)]

        def quantize_w(b, z0, z1):
            nc.vector.quantize_mx(out=codes[b][:, z0 * P:z1 * P].bitcast(FP8X4), scales=plane[b][:, z0 * P:z1 * P],
                                  in_=w_bf[b][:, z0:z1].rearrange("p z m t -> p (z m t)"))
            for z in range(z0, z1):
                w_codes[z, b] = codes[b][:, z * P:(z + 1) * P]
                w_plane[z, b] = plane[b][:, z * P:(z + 1) * P]

        gather_words(0, 0, BANK, "picked00")
        gather_words(0, BANK, BANK, "picked01")
        quantize_w(0, 0, 1)
        gather_words(1, 0, BANK, "w_raw0")
        quantize_w(0, 1, 2)
        gather_words(1, BANK, BANK // 2, "w_raw1")
        quantize_w(1, 0, 2)
        nc.vector.tensor_scalar(factor[:, V:2 * V], factor[:, 0:V], -1.0, 1.0, MULT, ADD)

        y = [sb.tile([P, S], F32, name=f"y{b}", align_bytes=64) for b in range(ROW_BLOCKS)]
        acc = {}

        def product(b, z, j0, n, bank=None):
            if z == 0:
                acc[b, j0] = psum.tile([P, BANK], F32, name=f"acc{b}_{j0}", tag=bank)
            nc.tensor.matmul_mx(out=acc[b, j0][:, 0:n],
                                lhsT=w_codes[z, b].bitcast(FP8X4), lhsT_scale=w_plane[z, b],
                                rhs=picked[z, j0 // BANK][:, j0 % BANK:j0 % BANK + n].bitcast(FP4X4), rhs_scale=x_plane[:, z, j0:j0 + n],
                                start=(z == 0), stop=(z == PASSES - 1))
            if z == PASSES - 1:
                nc.scalar.activation(y[b][:, j0:j0 + n], acc[b, j0][:, 0:n], GELU)

        for g, (j0, n) in enumerate(GROUPS):
            product(0, 0, j0, n, f"bank{g}")
        for j0, n in GROUPS:
            product(0, 1, j0, n)
        for g, (j0, n) in enumerate(WIDE):
            for z in range(PASSES):
                product(1, z, j0, n, f"bank{g}")

        def fetched(b, lst, c0, c1):
            return y[b][:].indirect(lst[:, c0 // STRIPE:c1 // STRIPE])

        term = [sb.tile([P, 2 * V], F32, name=f"term{b}", align_bytes=64) for b in range(ROW_BLOCKS)]
        res = [sb.tile([P, V], F32, name=f"res{b}", align_bytes=64) for b in range(ROW_BLOCKS)]
        plain = sb.tile([P, 2 * V], F32, name="plain", align_bytes=64)
        lent = sb.tile([P, LENT], F32, name="lent", tag="picked01", align_bytes=64)

        nc.scalar.activation(lent[:], fetched(0, left_t, 0, LENT), COPY)
        nc.scalar.activation(plain[:, OWN:V], fetched(1, right_t, OWN, V), COPY)
        nc.scalar.activation(plain[:, V:V + HALF], fetched(1, left_t, 0, HALF), COPY)
        nc.scalar.activation(plain[:, V + HALF:2 * V], fetched(1, left_t, HALF, V), COPY)

        nc.vector.tensor_tensor(term[0][:, 0:V], fetched(0, right_t, 0, V), factor[:, 0:V], MULT)
        nc.vector.tensor_tensor(term[0][:, V + LENT:2 * V], fetched(0, left_t, LENT, V), factor[:, V + LENT:2 * V], MULT)
        nc.vector.tensor_tensor(term[0][:, V:V + LENT], lent[:], factor[:, V:V + LENT], MULT)
        nc.vector.tensor_tensor(term[1][:, 0:OWN], fetched(1, right_t, 0, OWN), factor[:, 0:OWN], MULT)
        for c0, c1 in ((LENT, V), (0, LENT)):
            nc.vector.tensor_tensor(res[0][:, c0:c1], term[0][:, c0:c1], term[0][:, V + c0:V + c1], ADD)
        nc.sync.dma_start(out=out[0:P, :], in_=res[0][:])
        nc.vector.tensor_tensor(term[1][:, OWN:V + HALF], plain[:, OWN:V + HALF], factor[:, OWN:V + HALF], MULT)
        nc.vector.tensor_tensor(term[1][:, V + HALF:2 * V], plain[:, V + HALF:2 * V], factor[:, V + HALF:2 * V], MULT)
        for c0 in (0, HALF):
            nc.vector.tensor_tensor(res[1][:, c0:c0 + HALF], term[1][:, c0:c0 + HALF], term[1][:, V + c0:V + c0 + HALF], ADD)
            nc.sync.dma_start(out=out[P:2 * P, c0:c0 + HALF], in_=res[1][:, c0:c0 + HALF])
